import numpy as np
import ml_dtypes


def mxq(x, axis, fmt="e4m3"):
    dtype, down = {"e4m3": (ml_dtypes.float8_e4m3fn, 7), "e5m2": (ml_dtypes.float8_e5m2, 14)}[fmt]
    v = np.moveaxis(np.asarray(x, np.float32).astype(ml_dtypes.bfloat16).astype(np.float64), axis, -1)
    blocks = v.reshape(v.shape[:-1] + (-1, 32))
    amax = np.abs(blocks).max(-1, keepdims=True)
    byte = np.maximum(np.where(amax > 0, np.frexp(amax)[1] - 1 + 127, 0) - down, 1)
    scale = np.exp2(byte - 127.0)
    codes = (blocks / scale).astype(np.float32).astype(dtype).astype(np.float64)
    return np.moveaxis((codes * scale).reshape(v.shape), -1, axis)


WIDE = False


def mx_kscale(k):
    if not WIDE:
        return np.ones(k)
    levels = np.array([10, -10, 5, -5, 0])
    if k % 512:
        return np.exp2(np.random.permutation(np.resize(levels, k // 32))).repeat(32)
    a = np.empty((k // 512, 16))
    for p in range(k // 512):
        a[p, :8] = np.random.permutation(np.resize(levels, 8))
        for g in range(8):
            far = levels[np.abs(levels - a[p, g]) >= 10]
            a[p, g + 8] = far[np.random.randint(len(far))]
    return np.exp2(a.ravel()).repeat(32)


def f64(x):
    return np.asarray(x).astype(np.float64)


def striped(idx):
    return np.tile(idx.reshape(-1, 16).T, (8, 1)).astype(np.uint16)


def unstriped(offs):
    return offs[:16].T.reshape(-1).astype(np.int64)


def gelu(v):
    return 0.5 * v * (1.0 + np.tanh(np.sqrt(2.0 / np.pi) * (v + 0.044715 * v**3)))


K, T, D, S, V, N = 512, 2048, 4, 512, 256, 512


def setup_inputs():
    n = np.random.standard_normal
    s = mx_kscale(K)[:, None]
    return {
        "xT": (n((K, T)) * s).astype(np.float32),
        "w": (n((K, N)) / np.sqrt(K) / s).astype(np.float32),
        "b": (0.3 * n((N, 1))).astype(np.float32),
        "gate": np.tile(np.random.uniform(0.2, 1.0, (D, 1, V)) / np.sqrt(D), (1, N, 1)).astype(np.float32),
        "offs": striped(np.random.permutation(T)[:S]),
        "pos1": striped(np.random.permutation(S)[:V]),
        "pos2": striped(np.random.permutation(S)[:V]),
        "pos3": striped(np.random.permutation(S)[:V]),
        "pos4": striped(np.random.permutation(S)[:V]),
    }


def reference(xT, w, b, gate, offs, pos1, pos2, pos3, pos4):
    idx = unstriped(offs)
    xq = mxq(f64(xT)[:, idx], 0, "e4m3")
    y = mxq(f64(w), 0, "e4m3").T @ xq
    y = gelu(y + f64(b))
    return sum(f64(gate[d]) * y[:, unstriped(p)] for d, p in enumerate((pos1, pos2, pos3, pos4)))

@@ -1,0 +1,174 @@
+from contextlib import ExitStack
+
+import concourse.mybir as mybir
+from concourse.masks import make_identity
+
+K, T, D, S, V, N = 512, 2048, 4, 512, 256, 512
+FLOPS = 2 * K * N * S
+
+F32 = mybir.dt.float32
+BF16 = mybir.dt.bfloat16
+U32 = mybir.dt.uint32
+U16 = mybir.dt.uint16
+U8 = mybir.dt.uint8
+FP8X4 = mybir.dt.float8_e4m3fn_x4
+GELU = mybir.ActivationFunctionType.Gelu_apprx_tanh
+MULT = mybir.AluOpType.mult
+ADD = mybir.AluOpType.add
+
+P = 128
+PACK = 4
+BLOCKS = N // P
+HALF = S // 2
+PER_COLUMN = 16
+
+
+def tile_picked_sub_lin_gelu_sub_e_kernel(tc, xT, w, b, gate, offs, pos1, pos2, pos3, pos4, out):
+    nc = tc.nc
+    with ExitStack() as ctx:
+        lists = ctx.enter_context(tc.tile_pool(name="lists", bufs=1))
+        keep = ctx.enter_context(tc.tile_pool(name="keep", bufs=1))
+        psum = ctx.enter_context(tc.psum_pool(name="psum", bufs=2))
+
+        offs_t = lists.tile([P, S // PER_COLUMN], U16, name="offs_t")
+        pos_t = [lists.tile([P, V // PER_COLUMN], U16, name="pos_t%d" % d) for d in range(D)]
+        pos_in = [pos1, pos2, pos3, pos4]
+
+        x_raw = [keep.tile([P, T], F32, name="x_raw%d" % t) for t in range(PACK)]
+        w_raw = [keep.tile([P, PACK, P], F32, name="w_raw%d" % c) for c in range(BLOCKS)]
+        gates = [keep.tile([P, D, V], F32, name="gate%d" % c) for c in range(BLOCKS)]
+
+        x_rows = xT.rearrange("(p j) c -> p j c", j=PACK)
+        w_rows = w.rearrange("(p j) m -> p j m", j=PACK)
+        gate_rows = gate.rearrange("d m v -> m d v")
+
+        def load_w(c):
+            nc.sync.dma_start(out=w_raw[c][:], in_=w_rows[:, :, c * P : (c + 1) * P])
+
+        def load_gate(c):
+            nc.sync.dma_start(out=gates[c][:], in_=gate_rows[c * P : (c + 1) * P, :, :])
+
+        def load_pos(d):
+            nc.sync.dma_start(pos_t[d][:], pos_in[d])
+
+        b_rows = keep.tile([P, P], F32, name="b_rows")
+        nc.vector.memset(b_rows[:], 0.0)
+        nc.scalar.dma_start(out=b_rows[0:BLOCKS, :], in_=b.rearrange("(c m) o -> c (m o)", c=BLOCKS))
+
+        nc.sync.dma_start(out=x_raw[0][:], in_=x_rows[:, 0, :])
+        nc.sync.dma_start(offs_t[:], offs)
+        for d in range(D):
+            load_pos(d)
+        for t in range(1, PACK):
+            nc.sync.dma_start(out=x_raw[t][:], in_=x_rows[:, t, :])
+        load_w(0)
+        for c in range(BLOCKS):
+            if c + 1 < BLOCKS:
+                load_w(c + 1)
+            load_gate(c)
+
+        warm = keep.tile([P, 8], F32, name="warm")
+        warm_out = keep.tile([P, 8], F32, name="warm_out")
+        nc.vector.memset(warm[:], 0.0)
+        nc.scalar.activation(warm_out[:], warm[:], GELU)
+
+        ident = keep.tile([P, P], F32, name="ident")
+        make_identity(nc, ident[:])
+        b_turned = psum.tile([P, V], F32, name="b_turned", tag="back")
+        nc.tensor.transpose(b_turned[:, 0:P], b_rows[:], ident[:])
+        bias = keep.tile([P, BLOCKS], F32, name="bias")
+        nc.scalar.copy(bias[:], b_turned[:, 0:BLOCKS])
+
+        x_grp = [keep.tile([P, HALF, PACK], BF16, name="x_grp%d" % h, align_bytes=64) for h in range(2)]
+        cols = HALF // PER_COLUMN
+        for t in range(PACK):
+            for h in range(2):
+                nc.vector.tensor_copy(x_grp[h][:, :, t], x_raw[t][:].indirect(offs_t[:, h * cols : (h + 1) * cols]))
+
+        x_codes = keep.tile([P, S], U32, name="x_codes", align_bytes=64)
+        x_scales = keep.tile([P, S], U8, name="x_scales", align_bytes=64)
+        w_grp = [keep.tile([P, P, PACK], BF16, name="w_grp%d" % c, align_bytes=64) for c in range(BLOCKS)]
+        w_codes = [keep.tile([P, P], U32, name="w_codes%d" % c, align_bytes=64) for c in range(BLOCKS)]
+        w_scales = [keep.tile([P, P], U8, name="w_scales%d" % c, align_bytes=64) for c in range(BLOCKS)]
+        y = [keep.tile([P, S], F32, name="y%d" % c) for c in range(BLOCKS)]
+
+        def quantize_x(h):
+            nc.vector.quantize_mx(
+                out=x_codes[:, h * HALF : (h + 1) * HALF].bitcast(FP8X4),
+                scales=x_scales[:, h * HALF : (h + 1) * HALF],
+                in_=x_grp[h][:].rearrange("p s j -> p (s j)"),
+            )
+
+        def quantize_w(c):
+            nc.scalar.copy(
+                w_grp[c][:].rearrange("p (m i) j -> p m j i", i=4),
+                w_raw[c][:].rearrange("p j (m i) -> p m j i", i=4),
+            )
+            nc.vector.quantize_mx(
+                out=w_codes[c][:].bitcast(FP8X4),
+                scales=w_scales[c][:],
+                in_=w_grp[c][:].rearrange("p m j -> p (m j)"),
+            )
+
+        def layer(c, lo, hi):
+            acc = psum.tile([P, hi - lo], F32, name="acc", tag="acc")
+            nc.tensor.matmul_mx(
+                out=acc[:],
+                lhsT=w_codes[c][:].bitcast(FP8X4),
+                lhsT_scale=w_scales[c][:],
+                rhs=x_codes[:, lo:hi].bitcast(FP8X4),
+                rhs_scale=x_scales[:, lo:hi],
+                start=True,
+                stop=True,
+            )
+            nc.scalar.activation(y[c][:, lo:hi], acc[:], GELU, bias=bias[:, c : c + 1])
+
+        quantize_x(0)
+        quantize_w(0)
+        quantize_x(1)
+        layer(0, 0, HALF)
+        layer(0, HALF, S)
+        quantize_w(1)
+        layer(1, 0, S)
+
+        prod = [[keep.tile([P, V], F32, name="prod%d_%d" % (c, d)) for d in range(D)] for c in range(BLOCKS)]
+        result = [keep.tile([P, V], F32, name="result%d" % c) for c in range(BLOCKS)]
+
+        def fetch(c, d):
+            nc.vector.tensor_tensor(prod[c][d][:], y[c][:].indirect(pos_t[d][:]), gates[c][:, d, :], MULT)
+
+        def fetch_and_sum(c, turns):
+            turned = [psum.tile([P, P], F32, name="turned", tag="turned%d" % h) for h in range(2)]
+            for d in range(turns):
+                fetch(c, d)
+                for h in range(2):
+                    nc.tensor.matmul(
+                        turned[h][:],
+                        prod[c][d][:, h * P : (h + 1) * P],
+                        ident[:],
+                        start=(d == 0),
+                        stop=(d == turns - 1),
+                        is_transpose=True,
+                    )
+            back = psum.tile([P, V], F32, name="back", tag="back")
+            for h in range(2):
+                sums = keep.tile([P, P], F32, name="sums%d_%d" % (c, h))
+                nc.scalar.copy(sums[:], turned[h][:])
+                nc.tensor.transpose(back[:, h * P : (h + 1) * P], sums[:], ident[:])
+            return back
+
+        def store(c):
+            nc.sync.dma_start(out=out[c * P : (c + 1) * P, :], in_=result[c][:])
+
+        for c in range(2):
+            back = fetch_and_sum(c, D)
+            quantize_w(c + 2)
+            layer(c + 2, 0, S)
+            nc.scalar.copy(result[c][:], back[:])
+            store(c)
+        backs = [fetch_and_sum(c, D - 1) for c in (2, 3)]
+        for c in (2, 3):
+            fetch(c, D - 1)
+        for c in (2, 3):
+            nc.vector.tensor_tensor(result[c][:], prod[c][D - 1][:], backs[c - 2][:], ADD)
+            store(c)

@@ -35,7 +35,8 @@ def tile_picked_sub_lin_gelu_sub_e_kernel(tc, xT, w, b, gate, offs, pos1, pos2, 
         pos_in = [pos1, pos2, pos3, pos4]
 
         x_raw = [keep.tile([P, T], F32, name="x_raw%d" % t) for t in range(PACK)]
-        w_raw = [keep.tile([P, PACK, P], F32, name="w_raw%d" % c) for c in range(BLOCKS)]
+        spans = [(0, 1), (1, 3), (3, 4)]
+        w_raw = [keep.tile([P, PACK, (hi - lo) * P], F32, name="w_raw%d" % lo) for lo, hi in spans]
         gates = [keep.tile([P, D, V], F32, name="gate%d" % c) for c in range(BLOCKS)]
 
         x_rows = xT.rearrange("(p j) c -> p j c", j=PACK)
@@ -43,10 +44,10 @@ def tile_picked_sub_lin_gelu_sub_e_kernel(tc, xT, w, b, gate, offs, pos1, pos2, 
         gate_rows = gate.rearrange("d m v -> m d v")
 
         def load_w(c):
-            nc.sync.dma_start(out=w_raw[c][:], in_=w_rows[:, :, c * P : (c + 1) * P])
+            nc.sync.dma_start(out=w_raw[c][:], in_=w_rows[:, :, spans[c][0] * P : spans[c][1] * P])
 
-        def load_gate(c):
-            nc.sync.dma_start(out=gates[c][:], in_=gate_rows[c * P : (c + 1) * P, :, :])
+        def load_gate(c, lo, hi):
+            nc.sync.dma_start(out=gates[c][:, lo:hi, :], in_=gate_rows[c * P : (c + 1) * P, lo:hi, :])
 
         def load_pos(d):
             nc.sync.dma_start(pos_t[d][:], pos_in[d])
@@ -57,15 +58,17 @@ def tile_picked_sub_lin_gelu_sub_e_kernel(tc, xT, w, b, gate, offs, pos1, pos2, 
 
         nc.sync.dma_start(out=x_raw[0][:], in_=x_rows[:, 0, :])
         nc.sync.dma_start(offs_t[:], offs)
-        for d in range(D):
-            load_pos(d)
         for t in range(1, PACK):
             nc.sync.dma_start(out=x_raw[t][:], in_=x_rows[:, t, :])
         load_w(0)
-        for c in range(BLOCKS):
-            if c + 1 < BLOCKS:
-                load_w(c + 1)
-            load_gate(c)
+        load_w(1)
+        for lo in (0, 2):
+            load_pos(lo)
+            load_pos(lo + 1)
+            load_gate(0, lo, lo + 2)
+        load_w(2)
+        for c in range(1, BLOCKS):
+            load_gate(c, 0, D)
 
         warm = keep.tile([P, 8], F32, name="warm")
         warm_out = keep.tile([P, 8], F32, name="warm_out")
@@ -87,9 +90,9 @@ def tile_picked_sub_lin_gelu_sub_e_kernel(tc, xT, w, b, gate, offs, pos1, pos2, 
 
         x_codes = keep.tile([P, S], U32, name="x_codes", align_bytes=64)
         x_scales = keep.tile([P, S], U8, name="x_scales", align_bytes=64)
-        w_grp = [keep.tile([P, P, PACK], BF16, name="w_grp%d" % c, align_bytes=64) for c in range(BLOCKS)]
-        w_codes = [keep.tile([P, P], U32, name="w_codes%d" % c, align_bytes=64) for c in range(BLOCKS)]
-        w_scales = [keep.tile([P, P], U8, name="w_scales%d" % c, align_bytes=64) for c in range(BLOCKS)]
+        w_grp = [keep.tile([P, (hi - lo) * P, PACK], BF16, name="w_grp%d" % lo, align_bytes=64) for lo, hi in spans]
+        w_codes = keep.tile([P, N], U32, name="w_codes", align_bytes=64)
+        w_scales = keep.tile([P, N], U8, name="w_scales", align_bytes=64)
         y = [keep.tile([P, S], F32, name="y%d" % c) for c in range(BLOCKS)]
 
         def quantize_x(h):
@@ -100,13 +103,14 @@ def tile_picked_sub_lin_gelu_sub_e_kernel(tc, xT, w, b, gate, offs, pos1, pos2, 
             )
 
         def quantize_w(c):
-            nc.scalar.copy(
+            interleave = nc.vector.tensor_copy if c == 1 else nc.scalar.copy
+            interleave(
                 w_grp[c][:].rearrange("p (m i) j -> p m j i", i=4),
                 w_raw[c][:].rearrange("p j (m i) -> p m j i", i=4),
             )
             nc.vector.quantize_mx(
-                out=w_codes[c][:].bitcast(FP8X4),
-                scales=w_scales[c][:],
+                out=w_codes[:, spans[c][0] * P : spans[c][1] * P].bitcast(FP8X4),
+                scales=w_scales[:, spans[c][0] * P : spans[c][1] * P],
                 in_=w_grp[c][:].rearrange("p m j -> p (m j)"),
             )
 
@@ -114,8 +118,8 @@ def tile_picked_sub_lin_gelu_sub_e_kernel(tc, xT, w, b, gate, offs, pos1, pos2, 
             acc = psum.tile([P, hi - lo], F32, name="acc", tag="acc")
             nc.tensor.matmul_mx(
                 out=acc[:],
-                lhsT=w_codes[c][:].bitcast(FP8X4),
-                lhsT_scale=w_scales[c][:],
+                lhsT=w_codes[:, c * P : (c + 1) * P].bitcast(FP8X4),
+                lhsT_scale=w_scales[:, c * P : (c + 1) * P],
                 rhs=x_codes[:, lo:hi].bitcast(FP8X4),
                 rhs_scale=x_scales[:, lo:hi],
                 start=True,
@@ -134,14 +138,26 @@ def tile_picked_sub_lin_gelu_sub_e_kernel(tc, xT, w, b, gate, offs, pos1, pos2, 
         prod = [[keep.tile([P, V], F32, name="prod%d_%d" % (c, d)) for d in range(D)] for c in range(BLOCKS)]
         result = [keep.tile([P, V], F32, name="result%d" % c) for c in range(BLOCKS)]
 
+        def fetch_half(c, d, h):
+            nc.vector.tensor_tensor(
+                prod[c][d][:, h * P : (h + 1) * P],
+                y[c][:].indirect(pos_t[d][:, h * 8 : (h + 1) * 8]),
+                gates[c][:, d, h * P : (h + 1) * P],
+                MULT,
+            )
+
         def fetch(c, d):
             nc.vector.tensor_tensor(prod[c][d][:], y[c][:].indirect(pos_t[d][:]), gates[c][:, d, :], MULT)
 
         def fetch_and_sum(c, turns):
             turned = [psum.tile([P, P], F32, name="turned", tag="turned%d" % h) for h in range(2)]
             for d in range(turns):
-                fetch(c, d)
+                split = c == BLOCKS - 1 and d == turns - 1
+                if not split:
+                    fetch(c, d)
                 for h in range(2):
+                    if split:
+                        fetch_half(c, d, h)
                     nc.tensor.matmul(
                         turned[h][:],
                         prod[c][d][:, h * P : (h + 1) * P],
@@ -162,13 +178,19 @@ def tile_picked_sub_lin_gelu_sub_e_kernel(tc, xT, w, b, gate, offs, pos1, pos2, 
 
         for c in range(2):
             back = fetch_and_sum(c, D)
-            quantize_w(c + 2)
-            layer(c + 2, 0, S)
+            if c == 0:
+                layer(2, 0, S)
+                quantize_w(2)
+            else:
+                layer(3, 0, S)
             nc.scalar.copy(result[c][:], back[:])
             store(c)
         backs = [fetch_and_sum(c, D - 1) for c in (2, 3)]
         for c in (2, 3):
             fetch(c, D - 1)
-        for c in (2, 3):
-            nc.vector.tensor_tensor(result[c][:], prod[c][D - 1][:], backs[c - 2][:], ADD)
-            store(c)
+        nc.vector.tensor_tensor(result[2][:], prod[2][D - 1][:], backs[0][:], ADD)
+        store(2)
+        for h, queue in enumerate((nc.scalar, nc.sync)):
+            cut = slice(h * P, (h + 1) * P)
+            nc.vector.tensor_tensor(result[3][:, cut], prod[3][D - 1][:, cut], backs[1][:, cut], ADD)
+            queue.dma_start(out=out[3 * P : 4 * P, cut], in_=result[3][:, cut])

@@ -37,38 +37,30 @@ def tile_picked_sub_lin_gelu_sub_e_kernel(tc, xT, w, b, gate, offs, pos1, pos2, 
         x_raw = [keep.tile([P, T], F32, name="x_raw%d" % t) for t in range(PACK)]
         spans = [(0, 1), (1, 3), (3, 4)]
         w_raw = [keep.tile([P, PACK, (hi - lo) * P], F32, name="w_raw%d" % lo) for lo, hi in spans]
-        gates = [keep.tile([P, D, V], F32, name="gate%d" % c) for c in range(BLOCKS)]
 
         x_rows = xT.rearrange("(p j) c -> p j c", j=PACK)
         w_rows = w.rearrange("(p j) m -> p j m", j=PACK)
-        gate_rows = gate.rearrange("d m v -> m d v")
 
         def load_w(c):
             nc.sync.dma_start(out=w_raw[c][:], in_=w_rows[:, :, spans[c][0] * P : spans[c][1] * P])
 
-        def load_gate(c, lo, hi):
-            nc.sync.dma_start(out=gates[c][:, lo:hi, :], in_=gate_rows[c * P : (c + 1) * P, lo:hi, :])
-
         def load_pos(d):
             nc.sync.dma_start(pos_t[d][:], pos_in[d])
 
-        b_rows = keep.tile([P, P], F32, name="b_rows")
-        nc.vector.memset(b_rows[:], 0.0)
-        nc.scalar.dma_start(out=b_rows[0:BLOCKS, :], in_=b.rearrange("(c m) o -> c (m o)", c=BLOCKS))
+        rows = keep.tile([P, V], F32, name="rows")
+        nc.gpsimd.memset(rows[:], 0.0)
 
         nc.sync.dma_start(out=x_raw[0][:], in_=x_rows[:, 0, :])
         nc.sync.dma_start(offs_t[:], offs)
+        nc.sync.dma_start(out=rows[0:D, :], in_=gate[:, 0, :])
+        nc.sync.dma_start(out=rows[D : D + BLOCKS, 0:P], in_=b.rearrange("(c m) o -> c (m o)", c=BLOCKS))
         for t in range(1, PACK):
             nc.sync.dma_start(out=x_raw[t][:], in_=x_rows[:, t, :])
         load_w(0)
         load_w(1)
-        for lo in (0, 2):
-            load_pos(lo)
-            load_pos(lo + 1)
-            load_gate(0, lo, lo + 2)
         load_w(2)
-        for c in range(1, BLOCKS):
-            load_gate(c, 0, D)
+        for d in range(D):
+            load_pos(d)
 
         warm = keep.tile([P, 8], F32, name="warm")
         warm_out = keep.tile([P, 8], F32, name="warm_out")
@@ -77,10 +69,19 @@ def tile_picked_sub_lin_gelu_sub_e_kernel(tc, xT, w, b, gate, offs, pos1, pos2, 
 
         ident = keep.tile([P, P], F32, name="ident")
         make_identity(nc, ident[:])
-        b_turned = psum.tile([P, V], F32, name="b_turned", tag="back")
-        nc.tensor.transpose(b_turned[:, 0:P], b_rows[:], ident[:])
-        bias = keep.tile([P, BLOCKS], F32, name="bias")
-        nc.scalar.copy(bias[:], b_turned[:, 0:BLOCKS])
+        rows_turned = psum.tile([P, 2, P], F32, name="rows_turned", tag="back")
+        for h in range(2):
+            nc.tensor.transpose(rows_turned[:, h, :], rows[:, h * P : (h + 1) * P], ident[:])
+        consts = keep.tile([P, 2, D + BLOCKS], F32, name="consts")
+        nc.scalar.copy(consts[:], rows_turned[:, :, 0 : D + BLOCKS])
+        gates = [keep.tile([P, 2, V], F32, name="gates%d" % i) for i in range(2)]
+        for i in range(2):
+            spread = psum.tile([P, 2, V], F32, name="spread", tag="back")
+            for j in range(2):
+                for h in range(2):
+                    column = consts[:, h, 2 * i + j : 2 * i + j + 1].to_broadcast([P, P])
+                    nc.tensor.transpose(spread[:, j, h * P : (h + 1) * P], column, ident[:])
+            nc.scalar.copy(gates[i][:], spread[:])
 
         x_grp = [keep.tile([P, HALF, PACK], BF16, name="x_grp%d" % h, align_bytes=64) for h in range(2)]
         cols = HALF // PER_COLUMN
@@ -125,7 +126,7 @@ def tile_picked_sub_lin_gelu_sub_e_kernel(tc, xT, w, b, gate, offs, pos1, pos2, 
                 start=True,
                 stop=True,
             )
-            nc.scalar.activation(y[c][:, lo:hi], acc[:], GELU, bias=bias[:, c : c + 1])
+            nc.scalar.activation(y[c][:, lo:hi], acc[:], GELU, bias=consts[:, 0, D + c : D + c + 1])
 
         quantize_x(0)
         quantize_w(0)
@@ -134,6 +135,9 @@ def tile_picked_sub_lin_gelu_sub_e_kernel(tc, xT, w, b, gate, offs, pos1, pos2, 
         layer(0, HALF, S)
         quantize_w(1)
         layer(1, 0, S)
+        layer(2, 0, S)
+        quantize_w(2)
+        layer(3, 0, S)
 
         prod = [[keep.tile([P, V], F32, name="prod%d_%d" % (c, d)) for d in range(D)] for c in range(BLOCKS)]
         result = [keep.tile([P, V], F32, name="result%d" % c) for c in range(BLOCKS)]
@@ -142,12 +146,12 @@ def tile_picked_sub_lin_gelu_sub_e_kernel(tc, xT, w, b, gate, offs, pos1, pos2, 
             nc.vector.tensor_tensor(
                 prod[c][d][:, h * P : (h + 1) * P],
                 y[c][:].indirect(pos_t[d][:, h * 8 : (h + 1) * 8]),
-                gates[c][:, d, h * P : (h + 1) * P],
+                gates[d // 2][:, d % 2, h * P : (h + 1) * P],
                 MULT,
             )
 
         def fetch(c, d):
-            nc.vector.tensor_tensor(prod[c][d][:], y[c][:].indirect(pos_t[d][:]), gates[c][:, d, :], MULT)
+            nc.vector.tensor_tensor(prod[c][d][:], y[c][:].indirect(pos_t[d][:]), gates[d // 2][:, d % 2, :], MULT)
 
         def fetch_and_sum(c, turns):
             turned = [psum.tile([P, P], F32, name="turned", tag="turned%d" % h) for h in range(2)]
@@ -178,11 +182,6 @@ def tile_picked_sub_lin_gelu_sub_e_kernel(tc, xT, w, b, gate, offs, pos1, pos2, 
 
         for c in range(2):
             back = fetch_and_sum(c, D)
-            if c == 0:
-                layer(2, 0, S)
-                quantize_w(2)
-            else:
-                layer(3, 0, S)
             nc.scalar.copy(result[c][:], back[:])
             store(c)
         backs = [fetch_and_sum(c, D - 1) for c in (2, 3)]

@@ -36,7 +36,7 @@ def tile_picked_sub_lin_gelu_sub_e_kernel(tc, xT, w, b, gate, offs, pos1, pos2, 
 
         x_raw = [keep.tile([P, T], F32, name="x_raw%d" % t) for t in range(PACK)]
         spans = [(0, 1), (1, 3), (3, 4)]
-        w_raw = [keep.tile([P, PACK, (hi - lo) * P], F32, name="w_raw%d" % lo) for lo, hi in spans]
+        w_raw = [keep.tile([P, PACK, (hi - lo) * P], F32, name="w_raw%d" % lo, align_bytes=64) for lo, hi in spans]
 
         x_rows = xT.rearrange("(p j) c -> p j c", j=PACK)
         w_rows = w.rearrange("(p j) m -> p j m", j=PACK)
@@ -90,16 +90,18 @@ def tile_picked_sub_lin_gelu_sub_e_kernel(tc, xT, w, b, gate, offs, pos1, pos2, 
                 nc.vector.tensor_copy(x_grp[h][:, :, t], x_raw[t][:].indirect(offs_t[:, h * cols : (h + 1) * cols]))
 
         x_codes = keep.tile([P, S], U32, name="x_codes", align_bytes=64)
-        x_scales = keep.tile([P, S], U8, name="x_scales", align_bytes=64)
         w_grp = [keep.tile([P, (hi - lo) * P, PACK], BF16, name="w_grp%d" % lo, align_bytes=64) for lo, hi in spans]
         w_codes = keep.tile([P, N], U32, name="w_codes", align_bytes=64)
         w_scales = keep.tile([P, N], U8, name="w_scales", align_bytes=64)
         y = [keep.tile([P, S], F32, name="y%d" % c) for c in range(BLOCKS)]
 
+        x_scales = {}
+
         def quantize_x(h):
+            x_scales.setdefault(h, keep.tile([P, HALF], U8, name="x_scales%d" % h, tag=("x_scales", "w_raw0")[h], align_bytes=64))
             nc.vector.quantize_mx(
                 out=x_codes[:, h * HALF : (h + 1) * HALF].bitcast(FP8X4),
-                scales=x_scales[:, h * HALF : (h + 1) * HALF],
+                scales=x_scales[h][:],
                 in_=x_grp[h][:].rearrange("p s j -> p (s j)"),
             )
 
@@ -117,15 +119,16 @@ def tile_picked_sub_lin_gelu_sub_e_kernel(tc, xT, w, b, gate, offs, pos1, pos2, 
 
         def layer(c, lo, hi):
             acc = psum.tile([P, hi - lo], F32, name="acc", tag="acc")
-            nc.tensor.matmul_mx(
-                out=acc[:],
-                lhsT=w_codes[:, c * P : (c + 1) * P].bitcast(FP8X4),
-                lhsT_scale=w_scales[:, c * P : (c + 1) * P],
-                rhs=x_codes[:, lo:hi].bitcast(FP8X4),
-                rhs_scale=x_scales[:, lo:hi],
-                start=True,
-                stop=True,
-            )
+            for h in range(lo // HALF, hi // HALF):
+                nc.tensor.matmul_mx(
+                    out=acc[:, h * HALF - lo : (h + 1) * HALF - lo],
+                    lhsT=w_codes[:, c * P : (c + 1) * P].bitcast(FP8X4),
+                    lhsT_scale=w_scales[:, c * P : (c + 1) * P],
+                    rhs=x_codes[:, h * HALF : (h + 1) * HALF].bitcast(FP8X4),
+                    rhs_scale=x_scales[h][:],
+                    start=True,
+                    stop=True,
+                )
             nc.scalar.activation(y[c][:, lo:hi], acc[:], GELU, bias=consts[:, 0, D + c : D + c + 1])
 
         quantize_x(0)

@@ -58,8 +58,9 @@ def tile_picked_sub_lin_gelu_sub_e_kernel(tc, xT, w, b, gate, offs, pos1, pos2, 
             nc.sync.dma_start(out=x_raw[t][:], in_=x_rows[:, t, :])
         load_w(0)
         load_w(1)
+        load_pos(0)
         load_w(2)
-        for d in range(D):
+        for d in range(1, D):
             load_pos(d)
 
         warm = keep.tile([P, 8], F32, name="warm")
@@ -173,11 +174,15 @@ def tile_picked_sub_lin_gelu_sub_e_kernel(tc, xT, w, b, gate, offs, pos1, pos2, 
                         stop=(d == turns - 1),
                         is_transpose=True,
                     )
-            back = psum.tile([P, V], F32, name="back", tag="back")
+            if c == BLOCKS - 1:
+                back = [psum.tile([P, P], F32, name="back", tag="acc")[:] for h in range(2)]
+            else:
+                bank = psum.tile([P, V], F32, name="back", tag="back")
+                back = [bank[:, 0:P], bank[:, P:V], bank[:]]
             for h in range(2):
                 sums = keep.tile([P, P], F32, name="sums%d_%d" % (c, h))
                 nc.scalar.copy(sums[:], turned[h][:])
-                nc.tensor.transpose(back[:, h * P : (h + 1) * P], sums[:], ident[:])
+                nc.tensor.transpose(back[h], sums[:], ident[:])
             return back
 
         def store(c):
@@ -185,14 +190,14 @@ def tile_picked_sub_lin_gelu_sub_e_kernel(tc, xT, w, b, gate, offs, pos1, pos2, 
 
         for c in range(2):
             back = fetch_and_sum(c, D)
-            nc.scalar.copy(result[c][:], back[:])
+            nc.scalar.copy(result[c][:], back[2])
             store(c)
         backs = [fetch_and_sum(c, D - 1) for c in (2, 3)]
         for c in (2, 3):
             fetch(c, D - 1)
-        nc.vector.tensor_tensor(result[2][:], prod[2][D - 1][:], backs[0][:], ADD)
+        nc.vector.tensor_tensor(result[2][:], prod[2][D - 1][:], backs[0][2], ADD)
         store(2)
         for h, queue in enumerate((nc.scalar, nc.sync)):
             cut = slice(h * P, (h + 1) * P)
-            nc.vector.tensor_tensor(result[3][:, cut], prod[3][D - 1][:, cut], backs[1][:, cut], ADD)
+            nc.vector.tensor_tensor(result[3][:, cut], prod[3][D - 1][:, cut], backs[1][h], ADD)
             queue.dma_start(out=out[3 * P : 4 * P, cut], in_=result[3][:, cut])

@@ -35,7 +35,7 @@ def tile_picked_sub_lin_gelu_sub_e_kernel(tc, xT, w, b, gate, offs, pos1, pos2, 
         pos_in = [pos1, pos2, pos3, pos4]
 
         x_raw = [keep.tile([P, T], F32, name="x_raw%d" % t) for t in range(PACK)]
-        spans = [(0, 1), (1, 3), (3, 4)]
+        spans = [(0, 1), (1, 2), (2, 4)]
         w_raw = [keep.tile([P, PACK, (hi - lo) * P], F32, name="w_raw%d" % lo, align_bytes=64) for lo, hi in spans]
 
         x_rows = xT.rearrange("(p j) c -> p j c", j=PACK)
@@ -50,18 +50,18 @@ def tile_picked_sub_lin_gelu_sub_e_kernel(tc, xT, w, b, gate, offs, pos1, pos2, 
         rows = keep.tile([P, V], F32, name="rows")
         nc.gpsimd.memset(rows[:], 0.0)
 
+        nc.scalar.dma_start(out=w_raw[0][:], in_=w_rows[:, :, 0:P])
         nc.sync.dma_start(out=x_raw[0][:], in_=x_rows[:, 0, :])
         nc.sync.dma_start(offs_t[:], offs)
         nc.sync.dma_start(out=rows[0:D, :], in_=gate[:, 0, :])
         nc.sync.dma_start(out=rows[D : D + BLOCKS, 0:P], in_=b.rearrange("(c m) o -> c (m o)", c=BLOCKS))
         for t in range(1, PACK):
             nc.sync.dma_start(out=x_raw[t][:], in_=x_rows[:, t, :])
-        load_w(0)
+            if t < PACK - 1:
+                load_pos(2 * t - 2)
+                load_pos(2 * t - 1)
         load_w(1)
-        load_pos(0)
         load_w(2)
-        for d in range(1, D):
-            load_pos(d)
 
         warm = keep.tile([P, 8], F32, name="warm")
         warm_out = keep.tile([P, 8], F32, name="warm_out")
@@ -96,18 +96,18 @@ def tile_picked_sub_lin_gelu_sub_e_kernel(tc, xT, w, b, gate, offs, pos1, pos2, 
         w_scales = keep.tile([P, N], U8, name="w_scales", align_bytes=64)
         y = [keep.tile([P, S], F32, name="y%d" % c) for c in range(BLOCKS)]
 
-        x_scales = {}
+        x_scales = keep.tile([P, S], U8, name="x_scales", align_bytes=64)
 
-        def quantize_x(h):
-            x_scales.setdefault(h, keep.tile([P, HALF], U8, name="x_scales%d" % h, tag=("x_scales", "w_raw0")[h], align_bytes=64))
+        def quantize_x(q):
+            lo = q * P
             nc.vector.quantize_mx(
-                out=x_codes[:, h * HALF : (h + 1) * HALF].bitcast(FP8X4),
-                scales=x_scales[h][:],
-                in_=x_grp[h][:].rearrange("p s j -> p (s j)"),
+                out=x_codes[:, lo : lo + P].bitcast(FP8X4),
+                scales=x_scales[:, lo : lo + P],
+                in_=x_grp[q // 2][:, lo % HALF : lo % HALF + P, :].rearrange("p s j -> p (s j)"),
             )
 
         def quantize_w(c):
-            interleave = nc.vector.tensor_copy if c == 1 else nc.scalar.copy
+            interleave = nc.vector.tensor_copy if c == 2 else nc.scalar.copy
             interleave(
                 w_grp[c][:].rearrange("p (m i) j -> p m j i", i=4),
                 w_raw[c][:].rearrange("p j (m i) -> p m j i", i=4),
@@ -118,30 +118,30 @@ def tile_picked_sub_lin_gelu_sub_e_kernel(tc, xT, w, b, gate, offs, pos1, pos2, 
                 in_=w_grp[c][:].rearrange("p m j -> p (m j)"),
             )
 
-        def layer(c, lo, hi):
-            acc = psum.tile([P, hi - lo], F32, name="acc", tag="acc")
-            for h in range(lo // HALF, hi // HALF):
+        def layer(c, cuts, tag):
+            acc = psum.tile([P, cuts[-1] - cuts[0]], F32, name="acc", tag=tag)
+            for lo, hi in zip(cuts, cuts[1:]):
                 nc.tensor.matmul_mx(
-                    out=acc[:, h * HALF - lo : (h + 1) * HALF - lo],
+                    out=acc[:, lo - cuts[0] : hi - cuts[0]],
                     lhsT=w_codes[:, c * P : (c + 1) * P].bitcast(FP8X4),
                     lhsT_scale=w_scales[:, c * P : (c + 1) * P],
-                    rhs=x_codes[:, h * HALF : (h + 1) * HALF].bitcast(FP8X4),
-                    rhs_scale=x_scales[h][:],
+                    rhs=x_codes[:, lo:hi].bitcast(FP8X4),
+                    rhs_scale=x_scales[:, lo:hi],
                     start=True,
                     stop=True,
                 )
-            nc.scalar.activation(y[c][:, lo:hi], acc[:], GELU, bias=consts[:, 0, D + c : D + c + 1])
+            nc.scalar.activation(y[c][:, cuts[0] : cuts[-1]], acc[:], GELU, bias=consts[:, 0, D + c : D + c + 1])
 
-        quantize_x(0)
         quantize_w(0)
-        quantize_x(1)
-        layer(0, 0, HALF)
-        layer(0, HALF, S)
+        for q in range(4):
+            quantize_x(q)
+        for q in range(4):
+            layer(0, (q * P, (q + 1) * P), ("acc", "back")[q // 2])
         quantize_w(1)
-        layer(1, 0, S)
-        layer(2, 0, S)
         quantize_w(2)
-        layer(3, 0, S)
+        layer(1, (0, S), "acc")
+        layer(2, (0, S), "acc")
+        layer(3, (0, S), "acc")
 
         prod = [[keep.tile([P, V], F32, name="prod%d_%d" % (c, d)) for d in range(D)] for c in range(BLOCKS)]
         result = [keep.tile([P, V], F32, name="result%d" % c) for c in range(BLOCKS)]

@@ -53,20 +53,19 @@ def tile_picked_sub_lin_gelu_sub_e_kernel(tc, xT, w, b, gate, offs, pos1, pos2, 
         nc.scalar.dma_start(out=w_raw[0][:], in_=w_rows[:, :, 0:P])
         nc.sync.dma_start(out=x_raw[0][:], in_=x_rows[:, 0, :])
         nc.sync.dma_start(offs_t[:], offs)
-        nc.sync.dma_start(out=rows[0:D, :], in_=gate[:, 0, :])
-        nc.sync.dma_start(out=rows[D : D + BLOCKS, 0:P], in_=b.rearrange("(c m) o -> c (m o)", c=BLOCKS))
+        nc.scalar.dma_start(out=rows[0:D, :], in_=gate[:, 0, :])
+        nc.scalar.dma_start(out=rows[D : D + BLOCKS, 0:P], in_=b.rearrange("(c m) o -> c (m o)", c=BLOCKS))
         for t in range(1, PACK):
             nc.sync.dma_start(out=x_raw[t][:], in_=x_rows[:, t, :])
-            if t < PACK - 1:
-                load_pos(2 * t - 2)
-                load_pos(2 * t - 1)
+            if t == 1:
+                load_pos(0)
         load_w(1)
         load_w(2)
+        for d in range(1, D):
+            load_pos(d)
 
-        warm = keep.tile([P, 8], F32, name="warm")
         warm_out = keep.tile([P, 8], F32, name="warm_out")
-        nc.vector.memset(warm[:], 0.0)
-        nc.scalar.activation(warm_out[:], warm[:], GELU)
+        nc.scalar.activation(warm_out[:], w_raw[0][:, 0, 0:8], GELU)
 
         ident = keep.tile([P, P], F32, name="ident")
         make_identity(nc, ident[:])

@@ -21,6 +21,9 @@ PACK = 4
 BLOCKS = N // P
 HALF = S // 2
 PER_COLUMN = 16
+FIRST_CUTS = (0, 128, 256, 384, 448, 512)
+LAST_CUTS = (0, 896, 1536, 1920, 2048)
+COPY = mybir.ActivationFunctionType.Copy
 
 
 def tile_picked_sub_lin_gelu_sub_e_kernel(tc, xT, w, b, gate, offs, pos1, pos2, pos3, pos4, out):
@@ -55,10 +58,12 @@ def tile_picked_sub_lin_gelu_sub_e_kernel(tc, xT, w, b, gate, offs, pos1, pos2, 
         nc.sync.dma_start(offs_t[:], offs)
         nc.scalar.dma_start(out=rows[0:D, :], in_=gate[:, 0, :])
         nc.scalar.dma_start(out=rows[D : D + BLOCKS, 0:P], in_=b.rearrange("(c m) o -> c (m o)", c=BLOCKS))
-        for t in range(1, PACK):
+        for t in range(1, PACK - 1):
             nc.sync.dma_start(out=x_raw[t][:], in_=x_rows[:, t, :])
             if t == 1:
                 load_pos(0)
+        for lo, hi in zip(LAST_CUTS, LAST_CUTS[1:]):
+            nc.sync.dma_start(out=x_raw[PACK - 1][:, lo:hi], in_=x_rows[:, PACK - 1, lo:hi])
         load_w(1)
         load_w(2)
         for d in range(1, D):
@@ -85,35 +90,46 @@ def tile_picked_sub_lin_gelu_sub_e_kernel(tc, xT, w, b, gate, offs, pos1, pos2, 
 
         x_grp = [keep.tile([P, HALF, PACK], BF16, name="x_grp%d" % h, align_bytes=64) for h in range(2)]
         cols = HALF // PER_COLUMN
-        for t in range(PACK):
+        for t in range(PACK - 1):
             for h in range(2):
                 nc.vector.tensor_copy(x_grp[h][:, :, t], x_raw[t][:].indirect(offs_t[:, h * cols : (h + 1) * cols]))
+        last = PACK - 1
+        x_last = keep.tile([P, T], BF16, name="x_last")
+        for i, (lo, hi) in enumerate(zip(LAST_CUTS, LAST_CUTS[1:])):
+            cast = (nc.scalar.copy, nc.vector.tensor_copy, nc.vector.tensor_copy, nc.scalar.copy)[i]
+            cast(x_last[:, lo:hi], x_raw[last][:, lo:hi])
+        nc.vector.tensor_copy(x_grp[0][:, :, last], x_raw[last][:].indirect(offs_t[:, 0:cols]))
+        nc.scalar.activation(x_grp[1][:, :, last], x_last[:].indirect(offs_t[:, cols : 2 * cols]), COPY)
 
         x_codes = keep.tile([P, S], U32, name="x_codes", align_bytes=64)
-        w_grp = [keep.tile([P, (hi - lo) * P, PACK], BF16, name="w_grp%d" % lo, align_bytes=64) for lo, hi in spans]
-        w_codes = keep.tile([P, N], U32, name="w_codes", align_bytes=64)
-        w_scales = keep.tile([P, N], U8, name="w_scales", align_bytes=64)
+        w_codes = [keep.tile([P, P], U32, name="w_codes%d" % c, align_bytes=64) for c in range(BLOCKS)]
+        w_scales = [keep.tile([P, P], U8, name="w_scales%d" % c, align_bytes=64) for c in range(BLOCKS)]
+        w_grp = {}
         y = [keep.tile([P, S], F32, name="y%d" % c) for c in range(BLOCKS)]
 
         x_scales = keep.tile([P, S], U8, name="x_scales", align_bytes=64)
 
-        def quantize_x(q):
-            lo = q * P
+        def quantize_x(lo, hi):
             nc.vector.quantize_mx(
-                out=x_codes[:, lo : lo + P].bitcast(FP8X4),
-                scales=x_scales[:, lo : lo + P],
-                in_=x_grp[q // 2][:, lo % HALF : lo % HALF + P, :].rearrange("p s j -> p (s j)"),
+                out=x_codes[:, lo:hi].bitcast(FP8X4),
+                scales=x_scales[:, lo:hi],
+                in_=x_grp[lo // HALF][:, lo % HALF : lo % HALF + hi - lo, :].rearrange("p s j -> p (s j)"),
+            )
+
+        def interleave_w(c, slot):
+            load = min(c, 2)
+            lo = (c - load) * P
+            w_grp[c] = keep.tile([P, P, PACK], BF16, name="w_grp%d" % c, tag=slot, align_bytes=64)
+            interleave = nc.vector.tensor_copy if c == 1 else nc.scalar.copy
+            interleave(
+                w_grp[c][:].rearrange("p (m i) j -> p m j i", i=4),
+                w_raw[load][:, :, lo : lo + P].rearrange("p j (m i) -> p m j i", i=4),
             )
 
         def quantize_w(c):
-            interleave = nc.vector.tensor_copy if c == 2 else nc.scalar.copy
-            interleave(
-                w_grp[c][:].rearrange("p (m i) j -> p m j i", i=4),
-                w_raw[c][:].rearrange("p j (m i) -> p m j i", i=4),
-            )
             nc.vector.quantize_mx(
-                out=w_codes[:, spans[c][0] * P : spans[c][1] * P].bitcast(FP8X4),
-                scales=w_scales[:, spans[c][0] * P : spans[c][1] * P],
+                out=w_codes[c][:].bitcast(FP8X4),
+                scales=w_scales[c][:],
                 in_=w_grp[c][:].rearrange("p m j -> p (m j)"),
             )
 
@@ -122,8 +138,8 @@ def tile_picked_sub_lin_gelu_sub_e_kernel(tc, xT, w, b, gate, offs, pos1, pos2, 
             for lo, hi in zip(cuts, cuts[1:]):
                 nc.tensor.matmul_mx(
                     out=acc[:, lo - cuts[0] : hi - cuts[0]],
-                    lhsT=w_codes[:, c * P : (c + 1) * P].bitcast(FP8X4),
-                    lhsT_scale=w_scales[:, c * P : (c + 1) * P],
+                    lhsT=w_codes[c][:].bitcast(FP8X4),
+                    lhsT_scale=w_scales[c][:],
                     rhs=x_codes[:, lo:hi].bitcast(FP8X4),
                     rhs_scale=x_scales[:, lo:hi],
                     start=True,
@@ -131,16 +147,21 @@ def tile_picked_sub_lin_gelu_sub_e_kernel(tc, xT, w, b, gate, offs, pos1, pos2, 
                 )
             nc.scalar.activation(y[c][:, cuts[0] : cuts[-1]], acc[:], GELU, bias=consts[:, 0, D + c : D + c + 1])
 
+        interleave_w(0, "w_grp0")
         quantize_w(0)
-        for q in range(4):
-            quantize_x(q)
-        for q in range(4):
-            layer(0, (q * P, (q + 1) * P), ("acc", "back")[q // 2])
+        pieces = list(zip(FIRST_CUTS, FIRST_CUTS[1:]))
+        for lo, hi in pieces:
+            quantize_x(lo, hi)
+        for piece, tag in zip(pieces, ("acc", "acc", "back", "back", "turned0")):
+            layer(0, piece, tag)
+        interleave_w(1, "x_grp1")
         quantize_w(1)
-        quantize_w(2)
         layer(1, (0, S), "acc")
-        layer(2, (0, S), "acc")
-        layer(3, (0, S), "acc")
+        interleave_w(2, "w_codes0")
+        interleave_w(3, "w_scales0")
+        for c in (2, 3):
+            quantize_w(c)
+            layer(c, (0, S), "acc")
 
         prod = [[keep.tile([P, V], F32, name="prod%d_%d" % (c, d)) for d in range(D)] for c in range(BLOCKS)]
         result = [keep.tile([P, V], F32, name="result%d" % c) for c in range(BLOCKS)]

@@ -38,7 +38,7 @@ def tile_picked_sub_lin_gelu_sub_e_kernel(tc, xT, w, b, gate, offs, pos1, pos2, 
         pos_in = [pos1, pos2, pos3, pos4]
 
         x_raw = [keep.tile([P, T], F32, name="x_raw%d" % t) for t in range(PACK)]
-        spans = [(0, 1), (1, 2), (2, 4)]
+        spans = [(0, 1), (1, 3), (3, 4)]
         w_raw = [keep.tile([P, PACK, (hi - lo) * P], F32, name="w_raw%d" % lo, align_bytes=64) for lo, hi in spans]
 
         x_rows = xT.rearrange("(p j) c -> p j c", j=PACK)
@@ -117,8 +117,8 @@ def tile_picked_sub_lin_gelu_sub_e_kernel(tc, xT, w, b, gate, offs, pos1, pos2, 
             )
 
         def interleave_w(c, slot):
-            load = min(c, 2)
-            lo = (c - load) * P
+            load = (c + 1) // 2
+            lo = (c - spans[load][0]) * P
             w_grp[c] = keep.tile([P, P, PACK], BF16, name="w_grp%d" % c, tag=slot, align_bytes=64)
             interleave = nc.vector.tensor_copy if c == 1 else nc.scalar.copy
             interleave(
@@ -158,7 +158,7 @@ def tile_picked_sub_lin_gelu_sub_e_kernel(tc, xT, w, b, gate, offs, pos1, pos2, 
         quantize_w(1)
         layer(1, (0, S), "acc")
         interleave_w(2, "w_codes0")
-        interleave_w(3, "w_scales0")
+        interleave_w(3, "w_scales1")
         for c in (2, 3):
             quantize_w(c)
             layer(c, (0, S), "acc")

@@ -64,10 +64,11 @@ def tile_picked_sub_lin_gelu_sub_e_kernel(tc, xT, w, b, gate, offs, pos1, pos2, 
                 load_pos(0)
         for lo, hi in zip(LAST_CUTS, LAST_CUTS[1:]):
             nc.sync.dma_start(out=x_raw[PACK - 1][:, lo:hi], in_=x_rows[:, PACK - 1, lo:hi])
+        load_pos(1)
+        load_pos(2)
         load_w(1)
         load_w(2)
-        for d in range(1, D):
-            load_pos(d)
+        load_pos(3)
 
         warm_out = keep.tile([P, 8], F32, name="warm_out")
         nc.scalar.activation(warm_out[:], w_raw[0][:, 0, 0:8], GELU)
@@ -103,7 +104,7 @@ def tile_picked_sub_lin_gelu_sub_e_kernel(tc, xT, w, b, gate, offs, pos1, pos2, 
 
         x_codes = keep.tile([P, S], U32, name="x_codes", align_bytes=64)
         w_codes = [keep.tile([P, P], U32, name="w_codes%d" % c, align_bytes=64) for c in range(BLOCKS)]
-        w_scales = [keep.tile([P, P], U8, name="w_scales%d" % c, align_bytes=64) for c in range(BLOCKS)]
+        w_scales = [keep.tile([P, P], U8, name="w_scales%d" % c, align_bytes=64) for c in range(BLOCKS - 1)]
         w_grp = {}
         y = [keep.tile([P, S], F32, name="y%d" % c) for c in range(BLOCKS)]
 
@@ -119,10 +120,13 @@ def tile_picked_sub_lin_gelu_sub_e_kernel(tc, xT, w, b, gate, offs, pos1, pos2, 
         def interleave_w(c, slot):
             load = (c + 1) // 2
             lo = (c - spans[load][0]) * P
-            w_grp[c] = keep.tile([P, P, PACK], BF16, name="w_grp%d" % c, tag=slot, align_bytes=64)
-            interleave = nc.vector.tensor_copy if c == 1 else nc.scalar.copy
+            if c in (1, 2):
+                w_grp[c] = slot[:, c - 1]
+            else:
+                w_grp[c] = keep.tile([P, P, PACK], BF16, name="w_grp%d" % c, tag=slot, align_bytes=64)[:]
+            interleave = nc.vector.tensor_copy if c in (1, 2) else nc.scalar.copy
             interleave(
-                w_grp[c][:].rearrange("p (m i) j -> p m j i", i=4),
+                w_grp[c].rearrange("p (m i) j -> p m j i", i=4),
                 w_raw[load][:, :, lo : lo + P].rearrange("p j (m i) -> p m j i", i=4),
             )
 
@@ -130,7 +134,7 @@ def tile_picked_sub_lin_gelu_sub_e_kernel(tc, xT, w, b, gate, offs, pos1, pos2, 
             nc.vector.quantize_mx(
                 out=w_codes[c][:].bitcast(FP8X4),
                 scales=w_scales[c][:],
-                in_=w_grp[c][:].rearrange("p m j -> p (m j)"),
+                in_=w_grp[c].rearrange("p m j -> p (m j)"),
             )
 
         def layer(c, cuts, tag):
@@ -154,16 +158,22 @@ def tile_picked_sub_lin_gelu_sub_e_kernel(tc, xT, w, b, gate, offs, pos1, pos2, 
             quantize_x(lo, hi)
         for piece, tag in zip(pieces, ("acc", "acc", "back", "back", "turned0")):
             layer(0, piece, tag)
-        interleave_w(1, "x_grp1")
-        quantize_w(1)
-        layer(1, (0, S), "acc")
-        interleave_w(2, "w_codes0")
-        interleave_w(3, "w_scales1")
-        for c in (2, 3):
+        w_pair = keep.tile([P, 2, P, PACK], BF16, name="w_pair", tag="x_grp1", align_bytes=64)
+        for c in (1, 2):
+            interleave_w(c, w_pair)
+        for c in (1, 2):
             quantize_w(c)
+        interleave_w(3, "w_codes0")
+        layer(1, (0, S), "acc")
+        w_scales.append(keep.tile([P, P], U8, name="w_scales3", tag="w_scales1", align_bytes=64))
+        quantize_w(3)
+        for c in (2, 3):
             layer(c, (0, S), "acc")
 
-        prod = [[keep.tile([P, V], F32, name="prod%d_%d" % (c, d)) for d in range(D)] for c in range(BLOCKS)]
+        first = keep.tile([P, D, V], F32, name="first", tag="w_raw1", align_bytes=64)
+        prod = [[first[:, d] for d in range(D)]]
+        for c in range(1, BLOCKS):
+            prod.append([keep.tile([P, V], F32, name="prod%d_%d" % (c, d))[:] for d in range(D)])
         result = [keep.tile([P, V], F32, name="result%d" % c) for c in range(BLOCKS)]
 
         def fetch_half(c, d, h):
@@ -175,7 +185,7 @@ def tile_picked_sub_lin_gelu_sub_e_kernel(tc, xT, w, b, gate, offs, pos1, pos2, 
             )
 
         def fetch(c, d):
-            nc.vector.tensor_tensor(prod[c][d][:], y[c][:].indirect(pos_t[d][:]), gates[d // 2][:, d % 2, :], MULT)
+            nc.vector.tensor_tensor(prod[c][d], y[c][:].indirect(pos_t[d][:]), gates[d // 2][:, d % 2, :], MULT)
 
         def fetch_and_sum(c, turns):
             turned = [psum.tile([P, P], F32, name="turned", tag="turned%d" % h) for h in range(2)]
@@ -215,7 +225,7 @@ def tile_picked_sub_lin_gelu_sub_e_kernel(tc, xT, w, b, gate, offs, pos1, pos2, 
         backs = [fetch_and_sum(c, D - 1) for c in (2, 3)]
         for c in (2, 3):
             fetch(c, D - 1)
-        nc.vector.tensor_tensor(result[2][:], prod[2][D - 1][:], backs[0][2], ADD)
+        nc.vector.tensor_tensor(result[2][:], prod[2][D - 1], backs[0][2], ADD)
         store(2)
         for h, queue in enumerate((nc.scalar, nc.sync)):
             cut = slice(h * P, (h + 1) * P)

@@ -64,10 +64,10 @@ def tile_picked_sub_lin_gelu_sub_e_kernel(tc, xT, w, b, gate, offs, pos1, pos2, 
                 load_pos(0)
         for lo, hi in zip(LAST_CUTS, LAST_CUTS[1:]):
             nc.sync.dma_start(out=x_raw[PACK - 1][:, lo:hi], in_=x_rows[:, PACK - 1, lo:hi])
-        load_pos(1)
-        load_pos(2)
         load_w(1)
+        load_pos(1)
         load_w(2)
+        load_pos(2)
         load_pos(3)
 
         warm_out = keep.tile([P, 8], F32, name="warm_out")

@@ -23,6 +23,7 @@ HALF = S // 2
 PER_COLUMN = 16
 FIRST_CUTS = (0, 128, 256, 384, 448, 512)
 LAST_CUTS = (0, 896, 1536, 1920, 2048)
+FIRST_SPLIT = 1408
 COPY = mybir.ActivationFunctionType.Copy
 
 
@@ -53,17 +54,18 @@ def tile_picked_sub_lin_gelu_sub_e_kernel(tc, xT, w, b, gate, offs, pos1, pos2, 
         rows = keep.tile([P, V], F32, name="rows")
         nc.gpsimd.memset(rows[:], 0.0)
 
-        nc.scalar.dma_start(out=w_raw[0][:], in_=w_rows[:, :, 0:P])
-        nc.sync.dma_start(out=x_raw[0][:], in_=x_rows[:, 0, :])
+        nc.scalar.dma_start(out=x_raw[0][:, 0:FIRST_SPLIT], in_=x_rows[:, 0, 0:FIRST_SPLIT])
+        nc.sync.dma_start(out=x_raw[0][:, FIRST_SPLIT:T], in_=x_rows[:, 0, FIRST_SPLIT:T])
         nc.sync.dma_start(offs_t[:], offs)
-        nc.scalar.dma_start(out=rows[0:D, :], in_=gate[:, 0, :])
-        nc.scalar.dma_start(out=rows[D : D + BLOCKS, 0:P], in_=b.rearrange("(c m) o -> c (m o)", c=BLOCKS))
+        nc.sync.dma_start(out=rows[0:D, :], in_=gate[:, 0, :])
+        nc.sync.dma_start(out=rows[D : D + BLOCKS, 0:P], in_=b.rearrange("(c m) o -> c (m o)", c=BLOCKS))
         for t in range(1, PACK - 1):
             nc.sync.dma_start(out=x_raw[t][:], in_=x_rows[:, t, :])
             if t == 1:
                 load_pos(0)
         for lo, hi in zip(LAST_CUTS, LAST_CUTS[1:]):
             nc.sync.dma_start(out=x_raw[PACK - 1][:, lo:hi], in_=x_rows[:, PACK - 1, lo:hi])
+        load_w(0)
         load_w(1)
         load_pos(1)
         load_w(2)
@@ -71,7 +73,7 @@ def tile_picked_sub_lin_gelu_sub_e_kernel(tc, xT, w, b, gate, offs, pos1, pos2, 
         load_pos(3)
 
         warm_out = keep.tile([P, 8], F32, name="warm_out")
-        nc.scalar.activation(warm_out[:], w_raw[0][:, 0, 0:8], GELU)
+        nc.scalar.activation(warm_out[32:64, :], rows[32:64, 0:8], GELU)
 
         ident = keep.tile([P, P], F32, name="ident")
         make_identity(nc, ident[:])
@@ -108,7 +110,6 @@ def tile_picked_sub_lin_gelu_sub_e_kernel(tc, xT, w, b, gate, offs, pos1, pos2, 
         w_grp = {}
         y = [keep.tile([P, S], F32, name="y%d" % c) for c in range(BLOCKS)]
 
-        x_scales = keep.tile([P, S], U8, name="x_scales", align_bytes=64)
 
         def quantize_x(lo, hi):
             nc.vector.quantize_mx(
@@ -124,7 +125,7 @@ def tile_picked_sub_lin_gelu_sub_e_kernel(tc, xT, w, b, gate, offs, pos1, pos2, 
                 w_grp[c] = slot[:, c - 1]
             else:
                 w_grp[c] = keep.tile([P, P, PACK], BF16, name="w_grp%d" % c, tag=slot, align_bytes=64)[:]
-            interleave = nc.vector.tensor_copy if c in (1, 2) else nc.scalar.copy
+            interleave = nc.vector.tensor_copy if c < 3 else nc.scalar.copy
             interleave(
                 w_grp[c].rearrange("p (m i) j -> p m j i", i=4),
                 w_raw[load][:, :, lo : lo + P].rearrange("p j (m i) -> p m j i", i=4),
@@ -152,6 +153,7 @@ def tile_picked_sub_lin_gelu_sub_e_kernel(tc, xT, w, b, gate, offs, pos1, pos2, 
             nc.scalar.activation(y[c][:, cuts[0] : cuts[-1]], acc[:], GELU, bias=consts[:, 0, D + c : D + c + 1])
 
         interleave_w(0, "w_grp0")
+        x_scales = keep.tile([P, S], U8, name="x_scales", tag="w_raw0", align_bytes=64)
         quantize_w(0)
         pieces = list(zip(FIRST_CUTS, FIRST_CUTS[1:]))
         for lo, hi in pieces:

@@ -13,6 +13,7 @@ U16 = mybir.dt.uint16
 U8 = mybir.dt.uint8
 FP8X4 = mybir.dt.float8_e4m3fn_x4
 GELU = mybir.ActivationFunctionType.Gelu_apprx_tanh
+COPY = mybir.ActivationFunctionType.Copy
 MULT = mybir.AluOpType.mult
 ADD = mybir.AluOpType.add
 
@@ -24,7 +25,6 @@ PER_COLUMN = 16
 FIRST_CUTS = (0, 128, 256, 384, 448, 512)
 LAST_CUTS = (0, 896, 1536, 1920, 2048)
 FIRST_SPLIT = 1408
-COPY = mybir.ActivationFunctionType.Copy
 
 
 def tile_picked_sub_lin_gelu_sub_e_kernel(tc, xT, w, b, gate, offs, pos1, pos2, pos3, pos4, out):
@@ -32,7 +32,10 @@ def tile_picked_sub_lin_gelu_sub_e_kernel(tc, xT, w, b, gate, offs, pos1, pos2, 
     with ExitStack() as ctx:
         lists = ctx.enter_context(tc.tile_pool(name="lists", bufs=1))
         keep = ctx.enter_context(tc.tile_pool(name="keep", bufs=1))
-        psum = ctx.enter_context(tc.psum_pool(name="psum", bufs=2))
+        psum = ctx.enter_context(tc.psum_pool(name="psum", bufs=1))
+
+        def bank(number, shape):
+            return psum.tile(shape, F32, name="bank", tag="bank%d" % number)
 
         offs_t = lists.tile([P, S // PER_COLUMN], U16, name="offs_t")
         pos_t = [lists.tile([P, V // PER_COLUMN], U16, name="pos_t%d" % d) for d in range(D)]
@@ -77,14 +80,14 @@ def tile_picked_sub_lin_gelu_sub_e_kernel(tc, xT, w, b, gate, offs, pos1, pos2, 
 
         ident = keep.tile([P, P], F32, name="ident")
         make_identity(nc, ident[:])
-        rows_turned = psum.tile([P, 2, P], F32, name="rows_turned", tag="back")
+        rows_turned = bank(7, [P, 2, P])
         for h in range(2):
             nc.tensor.transpose(rows_turned[:, h, :], rows[:, h * P : (h + 1) * P], ident[:])
         consts = keep.tile([P, 2, D + BLOCKS], F32, name="consts")
         nc.scalar.copy(consts[:], rows_turned[:, :, 0 : D + BLOCKS])
         gates = [keep.tile([P, 2, V], F32, name="gates%d" % i) for i in range(2)]
         for i in range(2):
-            spread = psum.tile([P, 2, V], F32, name="spread", tag="back")
+            spread = bank(5 + i, [P, 2, V])
             for j in range(2):
                 for h in range(2):
                     column = consts[:, h, 2 * i + j : 2 * i + j + 1].to_broadcast([P, P])
@@ -106,10 +109,9 @@ def tile_picked_sub_lin_gelu_sub_e_kernel(tc, xT, w, b, gate, offs, pos1, pos2, 
 
         x_codes = keep.tile([P, S], U32, name="x_codes", align_bytes=64)
         w_codes = [keep.tile([P, P], U32, name="w_codes%d" % c, align_bytes=64) for c in range(BLOCKS)]
-        w_scales = [keep.tile([P, P], U8, name="w_scales%d" % c, align_bytes=64) for c in range(BLOCKS - 1)]
+        w_scales = [keep.tile([P, P], U8, name="w_scales%d" % c, align_bytes=64) for c in range(BLOCKS)]
         w_grp = {}
         y = [keep.tile([P, S], F32, name="y%d" % c) for c in range(BLOCKS)]
-
 
         def quantize_x(lo, hi):
             nc.vector.quantize_mx(
@@ -118,16 +120,12 @@ def tile_picked_sub_lin_gelu_sub_e_kernel(tc, xT, w, b, gate, offs, pos1, pos2, 
                 in_=x_grp[lo // HALF][:, lo % HALF : lo % HALF + hi - lo, :].rearrange("p s j -> p (s j)"),
             )
 
-        def interleave_w(c, slot):
+        def interleave_w(c, copy, into):
             load = (c + 1) // 2
             lo = (c - spans[load][0]) * P
-            if c in (1, 2):
-                w_grp[c] = slot[:, c - 1]
-            else:
-                w_grp[c] = keep.tile([P, P, PACK], BF16, name="w_grp%d" % c, tag=slot, align_bytes=64)[:]
-            interleave = nc.vector.tensor_copy if c < 3 else nc.scalar.copy
-            interleave(
-                w_grp[c].rearrange("p (m i) j -> p m j i", i=4),
+            w_grp[c] = into
+            copy(
+                into.rearrange("p (m i) j -> p m j i", i=4),
                 w_raw[load][:, :, lo : lo + P].rearrange("p j (m i) -> p m j i", i=4),
             )
 
@@ -138,98 +136,145 @@ def tile_picked_sub_lin_gelu_sub_e_kernel(tc, xT, w, b, gate, offs, pos1, pos2, 
                 in_=w_grp[c].rearrange("p m j -> p (m j)"),
             )
 
-        def layer(c, cuts, tag):
-            acc = psum.tile([P, cuts[-1] - cuts[0]], F32, name="acc", tag=tag)
-            for lo, hi in zip(cuts, cuts[1:]):
-                nc.tensor.matmul_mx(
-                    out=acc[:, lo - cuts[0] : hi - cuts[0]],
-                    lhsT=w_codes[c][:].bitcast(FP8X4),
-                    lhsT_scale=w_scales[c][:],
-                    rhs=x_codes[:, lo:hi].bitcast(FP8X4),
-                    rhs_scale=x_scales[:, lo:hi],
-                    start=True,
-                    stop=True,
-                )
-            nc.scalar.activation(y[c][:, cuts[0] : cuts[-1]], acc[:], GELU, bias=consts[:, 0, D + c : D + c + 1])
+        def product(c, lo, hi, number):
+            acc = bank(number, [P, hi - lo])
+            nc.tensor.matmul_mx(
+                out=acc[:],
+                lhsT=w_codes[c][:].bitcast(FP8X4),
+                lhsT_scale=w_scales[c][:],
+                rhs=x_codes[:, lo:hi].bitcast(FP8X4),
+                rhs_scale=x_scales[:, lo:hi],
+                start=True,
+                stop=True,
+            )
+            return acc
 
-        interleave_w(0, "w_grp0")
+        def activate(c, lo, hi, acc):
+            nc.scalar.activation(y[c][:, lo:hi], acc[:], GELU, bias=consts[:, 0, D + c : D + c + 1])
+
+        w_grp0 = keep.tile([P, P, PACK], BF16, name="w_grp0", align_bytes=64)
+        interleave_w(0, nc.vector.tensor_copy, w_grp0[:])
         x_scales = keep.tile([P, S], U8, name="x_scales", tag="w_raw0", align_bytes=64)
         quantize_w(0)
         pieces = list(zip(FIRST_CUTS, FIRST_CUTS[1:]))
         for lo, hi in pieces:
             quantize_x(lo, hi)
-        for piece, tag in zip(pieces, ("acc", "acc", "back", "back", "turned0")):
-            layer(0, piece, tag)
+        for i, (lo, hi) in enumerate(pieces):
+            activate(0, lo, hi, product(0, lo, hi, i))
         w_pair = keep.tile([P, 2, P, PACK], BF16, name="w_pair", tag="x_grp1", align_bytes=64)
         for c in (1, 2):
-            interleave_w(c, w_pair)
+            interleave_w(c, nc.vector.tensor_copy, w_pair[:, c - 1])
         for c in (1, 2):
             quantize_w(c)
-        interleave_w(3, "w_codes0")
-        layer(1, (0, S), "acc")
-        w_scales.append(keep.tile([P, P], U8, name="w_scales3", tag="w_scales1", align_bytes=64))
-        quantize_w(3)
-        for c in (2, 3):
-            layer(c, (0, S), "acc")
+        acc1 = product(1, 0, S, 5)
+        acc2 = product(2, 0, S, 6)
 
-        first = keep.tile([P, D, V], F32, name="first", tag="w_raw1", align_bytes=64)
-        prod = [[first[:, d] for d in range(D)]]
-        for c in range(1, BLOCKS):
-            prod.append([keep.tile([P, V], F32, name="prod%d_%d" % (c, d))[:] for d in range(D)])
-        result = [keep.tile([P, V], F32, name="result%d" % c) for c in range(BLOCKS)]
+        fetched = {}
 
-        def fetch_half(c, d, h):
-            nc.vector.tensor_tensor(
-                prod[c][d][:, h * P : (h + 1) * P],
-                y[c][:].indirect(pos_t[d][:, h * 8 : (h + 1) * 8]),
-                gates[d // 2][:, d % 2, h * P : (h + 1) * P],
-                MULT,
-            )
+        def fresh(c, d, tag=None):
+            fetched[c, d] = keep.tile([P, V], F32, name="fetched%d_%d" % (c, d), tag=tag or "fetched%d_%d" % (c, d))[:]
+            return fetched[c, d]
 
-        def fetch(c, d):
-            nc.vector.tensor_tensor(prod[c][d], y[c][:].indirect(pos_t[d][:]), gates[d // 2][:, d % 2, :], MULT)
+        def fetch_gated(c, d, into):
+            nc.vector.tensor_tensor(into, y[c][:].indirect(pos_t[d][:]), gates[d // 2][:, d % 2, :], MULT)
 
-        def fetch_and_sum(c, turns):
-            turned = [psum.tile([P, P], F32, name="turned", tag="turned%d" % h) for h in range(2)]
-            for d in range(turns):
-                split = c == BLOCKS - 1 and d == turns - 1
-                if not split:
-                    fetch(c, d)
+        def fetch_plain(c, d):
+            nc.scalar.activation(fresh(c, d), y[c][:].indirect(pos_t[d][:]), COPY)
+
+        def turn_sum(c, turns, numbers):
+            turned = [bank(number, [P, P]) for number in numbers]
+            for d in turns:
                 for h in range(2):
-                    if split:
-                        fetch_half(c, d, h)
                     nc.tensor.matmul(
                         turned[h][:],
-                        prod[c][d][:, h * P : (h + 1) * P],
+                        fetched[c, d][:, h * P : (h + 1) * P],
                         ident[:],
-                        start=(d == 0),
-                        stop=(d == turns - 1),
+                        start=(d == turns[0]),
+                        stop=(d == turns[-1]),
                         is_transpose=True,
                     )
-            if c == BLOCKS - 1:
-                back = [psum.tile([P, P], F32, name="back", tag="acc")[:] for h in range(2)]
-            else:
-                bank = psum.tile([P, V], F32, name="back", tag="back")
-                back = [bank[:, 0:P], bank[:, P:V], bank[:]]
+            return turned
+
+        def turn_plain(c, d, number):
+            turned = bank(number, [P, 2, P])
             for h in range(2):
-                sums = keep.tile([P, P], F32, name="sums%d_%d" % (c, h))
-                nc.scalar.copy(sums[:], turned[h][:])
-                nc.tensor.transpose(back[h], sums[:], ident[:])
-            return back
+                nc.tensor.transpose(turned[:, h, :], fetched[c, d][:, h * P : (h + 1) * P], ident[:])
+            return turned
+
+        def empty_sum(c, turned):
+            part = keep.tile([P, 2, P], F32, name="sum%d" % c)
+            for h in range(2):
+                nc.scalar.copy(part[:, h, :], turned[h][:])
+            return part
+
+        def empty_scaled(c, d, turned):
+            part = keep.tile([P, 2, P], F32, name="scaled%d_%d" % (c, d))
+            for h in range(2):
+                nc.scalar.activation(part[:, h, :], turned[:, h, :], COPY, scale=consts[:, h, d : d + 1])
+            return part
+
+        def turn_back(parts, targets):
+            for h in range(2):
+                for i, part in enumerate(parts):
+                    nc.tensor.matmul(
+                        targets[h], part[:, h, :], ident[:], start=(i == 0), stop=(i == len(parts) - 1), is_transpose=True
+                    )
+
+        result = [keep.tile([P, V], F32, name="result%d" % c) for c in range(BLOCKS)]
 
         def store(c):
             nc.sync.dma_start(out=out[c * P : (c + 1) * P, :], in_=result[c][:])
 
-        for c in range(2):
-            back = fetch_and_sum(c, D)
-            nc.scalar.copy(result[c][:], back[2])
-            store(c)
-        backs = [fetch_and_sum(c, D - 1) for c in (2, 3)]
-        for c in (2, 3):
-            fetch(c, D - 1)
-        nc.vector.tensor_tensor(result[2][:], prod[2][D - 1], backs[0][2], ADD)
+        first = keep.tile([P, D, V], F32, name="first", tag="w_raw1", align_bytes=64)
+        for d in range(D):
+            fetched[0, d] = first[:, d]
+
+        activate(1, 0, S, acc1)
+        fetch_gated(0, 0, fetched[0, 0])
+        fetch_plain(1, 0)
+        fetch_gated(0, 1, fetched[0, 1])
+        w_grp3 = keep.tile([P, P, PACK], BF16, name="w_grp3", align_bytes=64)
+        interleave_w(3, nc.scalar.copy, w_grp3[:])
+        activate(2, 0, S, acc2)
+        fetch_gated(0, 2, fetched[0, 2])
+        quantize_w(3)
+        acc3 = product(3, 0, S, 7)
+        fetch_gated(0, 3, fetched[0, 3])
+        turned0 = turn_sum(0, range(D), (0, 1))
+        fetch_plain(1, 1)
+        fetch_plain(1, 2)
+        turned1 = [turn_plain(1, d, 3 + d) for d in range(3)]
+        activate(3, 0, S, acc3)
+        fetch_gated(1, 3, fresh(1, 3))
+        sum0 = empty_sum(0, turned0)
+        back0 = bank(2, [P, V])
+        turn_back([sum0], [back0[:, 0:P], back0[:, P:V]])
+        for d in (1, 2):
+            fetch_gated(2, d, fresh(2, d))
+        turned2 = turn_sum(2, (1, 2), (0, 1))
+        scaled1 = [empty_scaled(1, d, turned1[d]) for d in range(3)]
+        back1 = bank(6, [P, V])
+        turn_back(scaled1, [back1[:, 0:P], back1[:, P:V]])
+        nc.scalar.copy(result[0][:], back0[:])
+        store(0)
+        fetch_plain(2, 0)
+        turned2a = turn_plain(2, 0, 3)
+        for d in range(3):
+            fetch_gated(3, d, fresh(3, d))
+        turned3 = turn_sum(3, range(3), (4, 5))
+        parts2 = [empty_sum(2, turned2), empty_scaled(2, 0, turned2a)]
+        back2 = bank(2, [P, V])
+        turn_back(parts2, [back2[:, 0:P], back2[:, P:V]])
+        sum3 = empty_sum(3, turned3)
+        back3 = [bank(7, [P, P])[:], bank(3, [P, P])[:]]
+        turn_back([sum3], back3)
+        fetch_gated(2, 3, fresh(2, 3, "fetched3_1"))
+        fetch_gated(3, 3, fresh(3, 3))
+        nc.vector.tensor_tensor(result[1][:], fetched[1, 3], back1[:], ADD)
+        store(1)
+        nc.vector.tensor_tensor(result[2][:], fetched[2, 3], back2[:], ADD)
         store(2)
         for h, queue in enumerate((nc.scalar, nc.sync)):
             cut = slice(h * P, (h + 1) * P)
-            nc.vector.tensor_tensor(result[3][:, cut], prod[3][D - 1][:, cut], backs[1][h], ADD)
+            nc.vector.tensor_tensor(result[3][:, cut], fetched[3, 3][:, cut], back3[h], ADD)
             queue.dma_start(out=out[3 * P : 4 * P, cut], in_=result[3][:, cut])

@@ -111,7 +111,7 @@ def tile_picked_sub_lin_gelu_sub_e_kernel(tc, xT, w, b, gate, offs, pos1, pos2, 
         w_codes = [keep.tile([P, P], U32, name="w_codes%d" % c, align_bytes=64) for c in range(BLOCKS)]
         w_scales = [keep.tile([P, P], U8, name="w_scales%d" % c, align_bytes=64) for c in range(BLOCKS)]
         w_grp = {}
-        y = [keep.tile([P, S], F32, name="y%d" % c) for c in range(BLOCKS)]
+        y = [keep.tile([P, S], F32, name="y%d" % c, align_bytes=64) for c in range(BLOCKS)]
 
         def quantize_x(lo, hi):
             nc.vector.quantize_mx(
@@ -178,103 +178,120 @@ def tile_picked_sub_lin_gelu_sub_e_kernel(tc, xT, w, b, gate, offs, pos1, pos2, 
         def fetch_gated(c, d, into):
             nc.vector.tensor_tensor(into, y[c][:].indirect(pos_t[d][:]), gates[d // 2][:, d % 2, :], MULT)
 
-        def fetch_plain(c, d):
-            nc.scalar.activation(fresh(c, d), y[c][:].indirect(pos_t[d][:]), COPY)
+        def fetch_plain(c, d, into):
+            fetched[c, d] = into
+            nc.scalar.activation(into, y[c][:].indirect(pos_t[d][:]), COPY)
 
-        def turn_sum(c, turns, numbers):
-            turned = [bank(number, [P, P]) for number in numbers]
+        def turn(target, source, first_pass, last_pass):
+            for h in range(2):
+                nc.tensor.matmul(
+                    target[:, h * P : (h + 1) * P],
+                    source[:, h * P : (h + 1) * P],
+                    ident[:],
+                    start=(first_pass and h == 0),
+                    stop=(last_pass and h == 1),
+                    is_transpose=True,
+                )
+
+        def turn_sum(c, turns, number):
+            turned = bank(number, [P, V])
             for d in turns:
-                for h in range(2):
-                    nc.tensor.matmul(
-                        turned[h][:],
-                        fetched[c, d][:, h * P : (h + 1) * P],
-                        ident[:],
-                        start=(d == turns[0]),
-                        stop=(d == turns[-1]),
-                        is_transpose=True,
-                    )
+                turn(turned, fetched[c, d], d == turns[0], d == turns[-1])
             return turned
 
-        def turn_plain(c, d, number):
-            turned = bank(number, [P, 2, P])
-            for h in range(2):
-                nc.tensor.transpose(turned[:, h, :], fetched[c, d][:, h * P : (h + 1) * P], ident[:])
-            return turned
-
-        def empty_sum(c, turned):
-            part = keep.tile([P, 2, P], F32, name="sum%d" % c)
-            for h in range(2):
-                nc.scalar.copy(part[:, h, :], turned[h][:])
+        def empty_sum(part, turned):
+            nc.scalar.copy(part, turned[:])
             return part
 
-        def empty_scaled(c, d, turned):
-            part = keep.tile([P, 2, P], F32, name="scaled%d_%d" % (c, d))
+        def empty_scaled(part, d, turned):
             for h in range(2):
-                nc.scalar.activation(part[:, h, :], turned[:, h, :], COPY, scale=consts[:, h, d : d + 1])
+                cut = slice(h * P, (h + 1) * P)
+                nc.scalar.activation(part[:, cut], turned[:, cut], COPY, scale=consts[:, h, d : d + 1])
             return part
 
-        def turn_back(parts, targets):
-            for h in range(2):
-                for i, part in enumerate(parts):
-                    nc.tensor.matmul(
-                        targets[h], part[:, h, :], ident[:], start=(i == 0), stop=(i == len(parts) - 1), is_transpose=True
-                    )
+        def turn_back(part, number):
+            back = bank(number, [P, V])
+            turn(back, part, True, True)
+            return back
 
-        result = [keep.tile([P, V], F32, name="result%d" % c) for c in range(BLOCKS)]
+        result = {c: keep.tile([P, V], F32, name="result%d" % c) for c in (1, 2)}
 
         def store(c):
             nc.sync.dma_start(out=out[c * P : (c + 1) * P, :], in_=result[c][:])
 
-        first = keep.tile([P, D, V], F32, name="first", tag="w_raw1", align_bytes=64)
-        for d in range(D):
-            fetched[0, d] = first[:, d]
+        first = keep.tile([P, 2, V], F32, name="first", tag="w_raw1", align_bytes=64)
+        for d in (1, 2):
+            fetched[0, d] = first[:, d - 1]
 
+        fetch_plain(0, 0, fresh(0, 0))
+        plain0 = [turn_sum(0, (0,), 0)]
         activate(1, 0, S, acc1)
-        fetch_gated(0, 0, fetched[0, 0])
-        fetch_plain(1, 0)
-        fetch_gated(0, 1, fetched[0, 1])
-        w_grp3 = keep.tile([P, P, PACK], BF16, name="w_grp3", align_bytes=64)
-        interleave_w(3, nc.scalar.copy, w_grp3[:])
+        fetch_plain(0, 3, fresh(0, 3))
+        plain0.append(turn_sum(0, (3,), 1))
+        extra = keep.tile([P, P], F32, name="extra")
+        nc.scalar.activation(extra[:], y[1][:].indirect(pos_t[0][:, 0:8]), COPY)
+        extra_turned = bank(4, [P, P])
+        nc.tensor.transpose(extra_turned[:], extra[:], ident[:])
         activate(2, 0, S, acc2)
-        fetch_gated(0, 2, fetched[0, 2])
+        for d in (1, 2):
+            fetch_gated(0, d, fetched[0, d])
+        turned0 = turn_sum(0, (1, 2), 2)
+        w_grp3 = keep.tile([P, P, PACK], BF16, name="w_grp3", tag="w_codes1", align_bytes=64)
+        interleave_w(3, nc.vector.tensor_copy, w_grp3[:])
+        rest = keep.tile([P, P], F32, name="rest")
+        nc.vector.tensor_tensor(rest[:], y[1][:].indirect(pos_t[0][:, 8:16]), gates[0][:, 0, P:V], MULT)
         quantize_w(3)
         acc3 = product(3, 0, S, 7)
-        fetch_gated(0, 3, fetched[0, 3])
-        turned0 = turn_sum(0, range(D), (0, 1))
-        fetch_plain(1, 1)
-        fetch_plain(1, 2)
-        turned1 = [turn_plain(1, d, 3 + d) for d in range(3)]
+        late = keep.tile([P, 8, V], F32, name="late", tag="x_codes", align_bytes=64)
         activate(3, 0, S, acc3)
-        fetch_gated(1, 3, fresh(1, 3))
-        sum0 = empty_sum(0, turned0)
-        back0 = bank(2, [P, V])
-        turn_back([sum0], [back0[:, 0:P], back0[:, P:V]])
+        fetch_plain(2, 0, late[:, 4])
+        plain2 = [turn_sum(2, (0,), 7)]
         for d in (1, 2):
-            fetch_gated(2, d, fresh(2, d))
-        turned2 = turn_sum(2, (1, 2), (0, 1))
-        scaled1 = [empty_scaled(1, d, turned1[d]) for d in range(3)]
-        back1 = bank(6, [P, V])
-        turn_back(scaled1, [back1[:, 0:P], back1[:, P:V]])
+            fetch_gated(1, d, fresh(1, d))
+        turned1 = bank(5, [P, V])
+        nc.tensor.matmul(turned1[:, P:V], rest[:], ident[:], start=True, stop=False, is_transpose=True)
+        for d in (1, 2):
+            turn(turned1, fetched[1, d], False, d == 2)
+        fetch_gated(1, 3, fresh(1, 3))
+        sum1 = keep.tile([P, V], F32, name="sum1")
+        extra_scaled = keep.tile([P, P], F32, name="extra_scaled", tag="w_scales3", align_bytes=64)
+        nc.scalar.activation(extra_scaled[:], extra_turned[:], COPY, scale=consts[:, 0, 0:1])
+        back1 = bank(4, [P, V])
+        nc.tensor.matmul(back1[:, 0:P], extra_scaled[:], ident[:], start=True, stop=False, is_transpose=True)
+        turn(back1, empty_sum(sum1[:], turned1), False, True)
+        back0 = bank(3, [P, V])
+        for i, d in enumerate((0, 3)):
+            turn(back0, empty_scaled(late[:, i], d, plain0[i]), i == 0, False)
+        turn(back0, empty_sum(late[:, 2], turned0), False, True)
+        fetch_plain(2, 1, late[:, 3])
+        plain2.append(turn_sum(2, (1,), 0))
+        fetch_plain(2, 2, late[:, 5])
+        plain2.append(turn_sum(2, (2,), 1))
+        back2 = [bank(number, [P, P]) for number in (6, 5)]
+        scaled2 = keep.tile([P, V], F32, name="scaled2", tag="w_codes3", align_bytes=64)
+        for d, part in enumerate((scaled2[:], late[:, 6], late[:, 7])):
+            empty_scaled(part, d, plain2[d])
+            for h in range(2):
+                nc.tensor.matmul(
+                    back2[h][:], part[:, h * P : (h + 1) * P], ident[:], start=(d == 0), stop=(d == 2), is_transpose=True
+                )
+        result[0] = keep.tile([P, V], F32, name="result0", tag="w_codes3", align_bytes=64)
         nc.scalar.copy(result[0][:], back0[:])
-        store(0)
-        fetch_plain(2, 0)
-        turned2a = turn_plain(2, 0, 3)
+        nc.scalar.dma_start(out=out[0:P, :], in_=result[0][:])
         for d in range(3):
             fetch_gated(3, d, fresh(3, d))
-        turned3 = turn_sum(3, range(3), (4, 5))
-        parts2 = [empty_sum(2, turned2), empty_scaled(2, 0, turned2a)]
-        back2 = bank(2, [P, V])
-        turn_back(parts2, [back2[:, 0:P], back2[:, P:V]])
-        sum3 = empty_sum(3, turned3)
-        back3 = [bank(7, [P, P])[:], bank(3, [P, P])[:]]
-        turn_back([sum3], back3)
-        fetch_gated(2, 3, fresh(2, 3, "fetched3_1"))
+        partial = [keep.tile([P, V], F32, name="partial%d" % i) for i in range(2)]
+        nc.vector.tensor_tensor(partial[0][:], fetched[3, 0], fetched[3, 1], ADD)
         fetch_gated(3, 3, fresh(3, 3))
+        nc.vector.tensor_tensor(partial[1][:], partial[0][:], fetched[3, 2], ADD)
         nc.vector.tensor_tensor(result[1][:], fetched[1, 3], back1[:], ADD)
         store(1)
-        nc.vector.tensor_tensor(result[2][:], fetched[2, 3], back2[:], ADD)
-        store(2)
+        closing = keep.tile([P, V], F32, name="closing", tag="sum1")
+        fetch_gated(2, 3, closing[:])
+        result[3] = keep.tile([P, V], F32, name="result3", tag="fetched1_3")
+        nc.vector.tensor_tensor(result[3][:], partial[1][:], fetched[3, 3], ADD)
+        store(3)
         for h, queue in enumerate((nc.scalar, nc.sync)):
             cut = slice(h * P, (h + 1) * P)
-            nc.vector.tensor_tensor(result[3][:, cut], fetched[3, 3][:, cut], back3[h], ADD)
-            queue.dma_start(out=out[3 * P : 4 * P, cut], in_=result[3][:, cut])
+            nc.vector.tensor_tensor(result[2][:, cut], closing[:, cut], back2[h][:], ADD)
+            queue.dma_start(out=out[2 * P : 3 * P, cut], in_=result[2][:, cut])

@@ -214,7 +214,7 @@ def tile_picked_sub_lin_gelu_sub_e_kernel(tc, xT, w, b, gate, offs, pos1, pos2, 
             turn(back, part, True, True)
             return back
 
-        result = {c: keep.tile([P, V], F32, name="result%d" % c) for c in (1, 2)}
+        result = [keep.tile([P, V], F32, name="result%d" % c) for c in range(BLOCKS - 1)]
 
         def store(c):
             nc.sync.dma_start(out=out[c * P : (c + 1) * P, :], in_=result[c][:])
@@ -230,8 +230,6 @@ def tile_picked_sub_lin_gelu_sub_e_kernel(tc, xT, w, b, gate, offs, pos1, pos2, 
         plain0.append(turn_sum(0, (3,), 1))
         extra = keep.tile([P, P], F32, name="extra")
         nc.scalar.activation(extra[:], y[1][:].indirect(pos_t[0][:, 0:8]), COPY)
-        extra_turned = bank(4, [P, P])
-        nc.tensor.transpose(extra_turned[:], extra[:], ident[:])
         activate(2, 0, S, acc2)
         for d in (1, 2):
             fetch_gated(0, d, fetched[0, d])
@@ -242,10 +240,12 @@ def tile_picked_sub_lin_gelu_sub_e_kernel(tc, xT, w, b, gate, offs, pos1, pos2, 
         nc.vector.tensor_tensor(rest[:], y[1][:].indirect(pos_t[0][:, 8:16]), gates[0][:, 0, P:V], MULT)
         quantize_w(3)
         acc3 = product(3, 0, S, 7)
-        late = keep.tile([P, 8, V], F32, name="late", tag="x_codes", align_bytes=64)
+        late = keep.tile([P, 9, V], F32, name="late", tag="x_codes", align_bytes=64)
+        fetch_plain(2, 0, fresh(2, 0))
         activate(3, 0, S, acc3)
-        fetch_plain(2, 0, late[:, 4])
-        plain2 = [turn_sum(2, (0,), 7)]
+        extra_turned = bank(7, [P, P])
+        nc.tensor.transpose(extra_turned[:], extra[:], ident[:])
+        plain2 = [turn_sum(2, (0,), 4)]
         for d in (1, 2):
             fetch_gated(1, d, fresh(1, d))
         turned1 = bank(5, [P, V])
@@ -256,9 +256,10 @@ def tile_picked_sub_lin_gelu_sub_e_kernel(tc, xT, w, b, gate, offs, pos1, pos2, 
         sum1 = keep.tile([P, V], F32, name="sum1")
         extra_scaled = keep.tile([P, P], F32, name="extra_scaled", tag="w_scales3", align_bytes=64)
         nc.scalar.activation(extra_scaled[:], extra_turned[:], COPY, scale=consts[:, 0, 0:1])
-        back1 = bank(4, [P, V])
+        empty_sum(sum1[:], turned1)
+        back1 = bank(5, [P, V])
         nc.tensor.matmul(back1[:, 0:P], extra_scaled[:], ident[:], start=True, stop=False, is_transpose=True)
-        turn(back1, empty_sum(sum1[:], turned1), False, True)
+        turn(back1, sum1[:], False, True)
         back0 = bank(3, [P, V])
         for i, d in enumerate((0, 3)):
             turn(back0, empty_scaled(late[:, i], d, plain0[i]), i == 0, False)
@@ -267,17 +268,11 @@ def tile_picked_sub_lin_gelu_sub_e_kernel(tc, xT, w, b, gate, offs, pos1, pos2, 
         plain2.append(turn_sum(2, (1,), 0))
         fetch_plain(2, 2, late[:, 5])
         plain2.append(turn_sum(2, (2,), 1))
-        back2 = [bank(number, [P, P]) for number in (6, 5)]
-        scaled2 = keep.tile([P, V], F32, name="scaled2", tag="w_codes3", align_bytes=64)
-        for d, part in enumerate((scaled2[:], late[:, 6], late[:, 7])):
-            empty_scaled(part, d, plain2[d])
-            for h in range(2):
-                nc.tensor.matmul(
-                    back2[h][:], part[:, h * P : (h + 1) * P], ident[:], start=(d == 0), stop=(d == 2), is_transpose=True
-                )
-        result[0] = keep.tile([P, V], F32, name="result0", tag="w_codes3", align_bytes=64)
+        back2 = bank(6, [P, V])
         nc.scalar.copy(result[0][:], back0[:])
-        nc.scalar.dma_start(out=out[0:P, :], in_=result[0][:])
+        store(0)
+        for d in range(3):
+            turn(back2, empty_scaled(late[:, 6 + d], d, plain2[d]), d == 0, d == 2)
         for d in range(3):
             fetch_gated(3, d, fresh(3, d))
         partial = [keep.tile([P, V], F32, name="partial%d" % i) for i in range(2)]
@@ -288,10 +283,10 @@ def tile_picked_sub_lin_gelu_sub_e_kernel(tc, xT, w, b, gate, offs, pos1, pos2, 
         store(1)
         closing = keep.tile([P, V], F32, name="closing", tag="sum1")
         fetch_gated(2, 3, closing[:])
-        result[3] = keep.tile([P, V], F32, name="result3", tag="fetched1_3")
+        result.append(keep.tile([P, V], F32, name="result3", tag="fetched1_3"))
         nc.vector.tensor_tensor(result[3][:], partial[1][:], fetched[3, 3], ADD)
         store(3)
         for h, queue in enumerate((nc.scalar, nc.sync)):
             cut = slice(h * P, (h + 1) * P)
-            nc.vector.tensor_tensor(result[2][:, cut], closing[:, cut], back2[h][:], ADD)
+            nc.vector.tensor_tensor(result[2][:, cut], closing[:, cut], back2[:, cut], ADD)
             queue.dma_start(out=out[2 * P : 3 * P, cut], in_=result[2][:, cut])

@@ -234,7 +234,7 @@ def tile_picked_sub_lin_gelu_sub_e_kernel(tc, xT, w, b, gate, offs, pos1, pos2, 
         for d in (1, 2):
             fetch_gated(0, d, fetched[0, d])
         turned0 = turn_sum(0, (1, 2), 2)
-        w_grp3 = keep.tile([P, P, PACK], BF16, name="w_grp3", tag="w_codes1", align_bytes=64)
+        w_grp3 = keep.tile([P, P, PACK], BF16, name="w_grp3", tag="x_grp1", align_bytes=64)
         interleave_w(3, nc.vector.tensor_copy, w_grp3[:])
         rest = keep.tile([P, P], F32, name="rest")
         nc.vector.tensor_tensor(rest[:], y[1][:].indirect(pos_t[0][:, 8:16]), gates[0][:, 0, P:V], MULT)
@@ -286,7 +286,7 @@ def tile_picked_sub_lin_gelu_sub_e_kernel(tc, xT, w, b, gate, offs, pos1, pos2, 
         result.append(keep.tile([P, V], F32, name="result3", tag="fetched1_3"))
         nc.vector.tensor_tensor(result[3][:], partial[1][:], fetched[3, 3], ADD)
         store(3)
-        for h, queue in enumerate((nc.scalar, nc.sync)):
+        for h in range(2):
             cut = slice(h * P, (h + 1) * P)
             nc.vector.tensor_tensor(result[2][:, cut], closing[:, cut], back2[:, cut], ADD)
-            queue.dma_start(out=out[2 * P : 3 * P, cut], in_=result[2][:, cut])
+            nc.sync.dma_start(out=out[2 * P : 3 * P, cut], in_=result[2][:, cut])

@@ -22,8 +22,6 @@ PACK = 4
 BLOCKS = N // P
 HALF = S // 2
 PER_COLUMN = 16
-FIRST_CUTS = (0, 128, 256, 384, 448, 512)
-LAST_CUTS = (0, 896, 1536, 1920, 2048)
 FIRST_SPLIT = 1408
 
 
@@ -37,55 +35,55 @@ def tile_picked_sub_lin_gelu_sub_e_kernel(tc, xT, w, b, gate, offs, pos1, pos2, 
         def bank(number, shape):
             return psum.tile(shape, F32, name="bank", tag="bank%d" % number)
 
+        def sbuf(name, shape, dtype=F32, tag=None):
+            return keep.tile(shape, dtype, name=name, tag=tag or name, align_bytes=64)
+
         offs_t = lists.tile([P, S // PER_COLUMN], U16, name="offs_t")
         pos_t = [lists.tile([P, V // PER_COLUMN], U16, name="pos_t%d" % d) for d in range(D)]
         pos_in = [pos1, pos2, pos3, pos4]
 
-        x_raw = [keep.tile([P, T], F32, name="x_raw%d" % t) for t in range(PACK)]
-        spans = [(0, 1), (1, 3), (3, 4)]
-        w_raw = [keep.tile([P, PACK, (hi - lo) * P], F32, name="w_raw%d" % lo, align_bytes=64) for lo, hi in spans]
-
+        x_raw = [sbuf("x_raw%d" % t, [P, T]) for t in range(PACK)]
+        w_raw = [sbuf("w_raw%d" % c, [P, PACK, P]) for c in range(BLOCKS)]
         x_rows = xT.rearrange("(p j) c -> p j c", j=PACK)
         w_rows = w.rearrange("(p j) m -> p j m", j=PACK)
 
         def load_w(c):
-            nc.sync.dma_start(out=w_raw[c][:], in_=w_rows[:, :, spans[c][0] * P : spans[c][1] * P])
+            nc.sync.dma_start(out=w_raw[c][:], in_=w_rows[:, :, c * P : (c + 1) * P])
 
         def load_pos(d):
             nc.sync.dma_start(pos_t[d][:], pos_in[d])
 
-        rows = keep.tile([P, V], F32, name="rows")
+        rows = sbuf("rows", [P, V])
         nc.gpsimd.memset(rows[:], 0.0)
 
         nc.scalar.dma_start(out=x_raw[0][:, 0:FIRST_SPLIT], in_=x_rows[:, 0, 0:FIRST_SPLIT])
         nc.sync.dma_start(out=x_raw[0][:, FIRST_SPLIT:T], in_=x_rows[:, 0, FIRST_SPLIT:T])
         nc.sync.dma_start(offs_t[:], offs)
+        nc.sync.dma_start(out=x_raw[1][:], in_=x_rows[:, 1, :])
         nc.sync.dma_start(out=rows[0:D, :], in_=gate[:, 0, :])
         nc.sync.dma_start(out=rows[D : D + BLOCKS, 0:P], in_=b.rearrange("(c m) o -> c (m o)", c=BLOCKS))
-        for t in range(1, PACK - 1):
-            nc.sync.dma_start(out=x_raw[t][:], in_=x_rows[:, t, :])
-            if t == 1:
-                load_pos(0)
-        for lo, hi in zip(LAST_CUTS, LAST_CUTS[1:]):
-            nc.sync.dma_start(out=x_raw[PACK - 1][:, lo:hi], in_=x_rows[:, PACK - 1, lo:hi])
+        nc.sync.dma_start(out=x_raw[2][:], in_=x_rows[:, 2, :])
+        nc.sync.dma_start(out=x_raw[3][:], in_=x_rows[:, 3, :])
+        load_pos(0)
         load_w(0)
         load_w(1)
-        load_pos(1)
         load_w(2)
+        load_w(3)
+        load_pos(1)
         load_pos(2)
         load_pos(3)
 
-        warm_out = keep.tile([P, 8], F32, name="warm_out")
+        warm_out = sbuf("warm_out", [P, 8])
         nc.scalar.activation(warm_out[32:64, :], rows[32:64, 0:8], GELU)
 
-        ident = keep.tile([P, P], F32, name="ident")
+        ident = sbuf("ident", [P, P])
         make_identity(nc, ident[:])
         rows_turned = bank(7, [P, 2, P])
         for h in range(2):
             nc.tensor.transpose(rows_turned[:, h, :], rows[:, h * P : (h + 1) * P], ident[:])
-        consts = keep.tile([P, 2, D + BLOCKS], F32, name="consts")
+        consts = sbuf("consts", [P, 2, D + BLOCKS])
         nc.scalar.copy(consts[:], rows_turned[:, :, 0 : D + BLOCKS])
-        gates = [keep.tile([P, 2, V], F32, name="gates%d" % i) for i in range(2)]
+        gates = [sbuf("gates%d" % i, [P, 2, V]) for i in range(2)]
         for i in range(2):
             spread = bank(5 + i, [P, 2, V])
             for j in range(2):
@@ -94,24 +92,17 @@ def tile_picked_sub_lin_gelu_sub_e_kernel(tc, xT, w, b, gate, offs, pos1, pos2, 
                     nc.tensor.transpose(spread[:, j, h * P : (h + 1) * P], column, ident[:])
             nc.scalar.copy(gates[i][:], spread[:])
 
-        x_grp = [keep.tile([P, HALF, PACK], BF16, name="x_grp%d" % h, align_bytes=64) for h in range(2)]
+        x_grp = [sbuf("x_grp%d" % h, [P, HALF, PACK], BF16) for h in range(2)]
         cols = HALF // PER_COLUMN
-        for t in range(PACK - 1):
-            for h in range(2):
-                nc.vector.tensor_copy(x_grp[h][:, :, t], x_raw[t][:].indirect(offs_t[:, h * cols : (h + 1) * cols]))
-        last = PACK - 1
-        x_last = keep.tile([P, T], BF16, name="x_last")
-        for i, (lo, hi) in enumerate(zip(LAST_CUTS, LAST_CUTS[1:])):
-            cast = (nc.scalar.copy, nc.vector.tensor_copy, nc.vector.tensor_copy, nc.scalar.copy)[i]
-            cast(x_last[:, lo:hi], x_raw[last][:, lo:hi])
-        nc.vector.tensor_copy(x_grp[0][:, :, last], x_raw[last][:].indirect(offs_t[:, 0:cols]))
-        nc.scalar.activation(x_grp[1][:, :, last], x_last[:].indirect(offs_t[:, cols : 2 * cols]), COPY)
+        for t in range(PACK):
+            nc.vector.tensor_copy(x_grp[0][:, :, t], x_raw[t][:].indirect(offs_t[:, 0:cols]))
+            nc.scalar.activation(x_grp[1][:, :, t], x_raw[t][:].indirect(offs_t[:, cols : 2 * cols]), COPY)
 
-        x_codes = keep.tile([P, S], U32, name="x_codes", align_bytes=64)
-        w_codes = [keep.tile([P, P], U32, name="w_codes%d" % c, align_bytes=64) for c in range(BLOCKS)]
-        w_scales = [keep.tile([P, P], U8, name="w_scales%d" % c, align_bytes=64) for c in range(BLOCKS)]
+        x_codes = sbuf("x_codes", [P, S], U32)
+        w_codes = [sbuf("w_codes%d" % c, [P, P], U32) for c in range(BLOCKS)]
+        w_scales = [sbuf("w_scales%d" % c, [P, P], U8) for c in range(BLOCKS)]
         w_grp = {}
-        y = [keep.tile([P, S], F32, name="y%d" % c, align_bytes=64) for c in range(BLOCKS)]
+        y = [sbuf("y%d" % c, [P, S]) for c in range(BLOCKS)]
 
         def quantize_x(lo, hi):
             nc.vector.quantize_mx(
@@ -120,20 +111,17 @@ def tile_picked_sub_lin_gelu_sub_e_kernel(tc, xT, w, b, gate, offs, pos1, pos2, 
                 in_=x_grp[lo // HALF][:, lo % HALF : lo % HALF + hi - lo, :].rearrange("p s j -> p (s j)"),
             )
 
-        def interleave_w(c, copy, into):
-            load = (c + 1) // 2
-            lo = (c - spans[load][0]) * P
-            w_grp[c] = into
+        def interleave_w(c, lo, hi, copy):
             copy(
-                into.rearrange("p (m i) j -> p m j i", i=4),
-                w_raw[load][:, :, lo : lo + P].rearrange("p j (m i) -> p m j i", i=4),
+                w_grp[c][:, lo:hi, :].rearrange("p (m i) j -> p m j i", i=4),
+                w_raw[c][:, :, lo:hi].rearrange("p j (m i) -> p m j i", i=4),
             )
 
-        def quantize_w(c):
+        def quantize_w(c, lo, hi):
             nc.vector.quantize_mx(
-                out=w_codes[c][:].bitcast(FP8X4),
-                scales=w_scales[c][:],
-                in_=w_grp[c].rearrange("p m j -> p (m j)"),
+                out=w_codes[c][:, lo:hi].bitcast(FP8X4),
+                scales=w_scales[c][:, lo:hi],
+                in_=w_grp[c][:, lo:hi, :].rearrange("p m j -> p (m j)"),
             )
 
         def product(c, lo, hi, number):
@@ -152,141 +140,129 @@ def tile_picked_sub_lin_gelu_sub_e_kernel(tc, xT, w, b, gate, offs, pos1, pos2, 
         def activate(c, lo, hi, acc):
             nc.scalar.activation(y[c][:, lo:hi], acc[:], GELU, bias=consts[:, 0, D + c : D + c + 1])
 
-        w_grp0 = keep.tile([P, P, PACK], BF16, name="w_grp0", align_bytes=64)
-        interleave_w(0, nc.vector.tensor_copy, w_grp0[:])
-        x_scales = keep.tile([P, S], U8, name="x_scales", tag="w_raw0", align_bytes=64)
-        quantize_w(0)
-        pieces = list(zip(FIRST_CUTS, FIRST_CUTS[1:]))
-        for lo, hi in pieces:
-            quantize_x(lo, hi)
-        for i, (lo, hi) in enumerate(pieces):
-            activate(0, lo, hi, product(0, lo, hi, i))
-        w_pair = keep.tile([P, 2, P, PACK], BF16, name="w_pair", tag="x_grp1", align_bytes=64)
-        for c in (1, 2):
-            interleave_w(c, nc.vector.tensor_copy, w_pair[:, c - 1])
-        for c in (1, 2):
-            quantize_w(c)
-        acc1 = product(1, 0, S, 5)
-        acc2 = product(2, 0, S, 6)
-
-        fetched = {}
-
-        def fresh(c, d, tag=None):
-            fetched[c, d] = keep.tile([P, V], F32, name="fetched%d_%d" % (c, d), tag=tag or "fetched%d_%d" % (c, d))[:]
-            return fetched[c, d]
-
-        def fetch_gated(c, d, into):
-            nc.vector.tensor_tensor(into, y[c][:].indirect(pos_t[d][:]), gates[d // 2][:, d % 2, :], MULT)
+        def fetch_gated(c, d, into, lo=0, hi=V):
+            offsets = pos_t[d][:, lo // PER_COLUMN : hi // PER_COLUMN]
+            nc.vector.tensor_tensor(into[:, lo:hi], y[c][:].indirect(offsets), gates[d // 2][:, d % 2, lo:hi], MULT)
+            return into
 
         def fetch_plain(c, d, into):
-            fetched[c, d] = into
             nc.scalar.activation(into, y[c][:].indirect(pos_t[d][:]), COPY)
+            return into
+
+        def turn_half(target, source, h, start, stop):
+            nc.tensor.matmul(target, source[:, h * P : (h + 1) * P], ident[:], start=start, stop=stop, is_transpose=True)
 
         def turn(target, source, first_pass, last_pass):
             for h in range(2):
-                nc.tensor.matmul(
-                    target[:, h * P : (h + 1) * P],
-                    source[:, h * P : (h + 1) * P],
-                    ident[:],
-                    start=(first_pass and h == 0),
-                    stop=(last_pass and h == 1),
-                    is_transpose=True,
-                )
+                turn_half(target[:, h * P : (h + 1) * P], source, h, first_pass and h == 0, last_pass and h == 1)
 
-        def turn_sum(c, turns, number):
-            turned = bank(number, [P, V])
-            for d in turns:
-                turn(turned, fetched[c, d], d == turns[0], d == turns[-1])
-            return turned
+        def turned(source, number):
+            target = bank(number, [P, V])
+            turn(target, source, True, True)
+            return target
 
-        def empty_sum(part, turned):
-            nc.scalar.copy(part, turned[:])
-            return part
-
-        def empty_scaled(part, d, turned):
+        def scaled(d, source, into):
             for h in range(2):
                 cut = slice(h * P, (h + 1) * P)
-                nc.scalar.activation(part[:, cut], turned[:, cut], COPY, scale=consts[:, h, d : d + 1])
-            return part
+                nc.scalar.activation(into[:, cut], source[:, cut], COPY, scale=consts[:, h, d : d + 1])
+            return into
 
-        def turn_back(part, number):
-            back = bank(number, [P, V])
-            turn(back, part, True, True)
-            return back
+        def row(name, tag=None):
+            return sbuf(name, [P, V], F32, tag)[:]
 
-        result = [keep.tile([P, V], F32, name="result%d" % c) for c in range(BLOCKS - 1)]
+        def add(into, first, second):
+            nc.vector.tensor_tensor(into, first, second, ADD)
+            return into
 
-        def store(c):
-            nc.sync.dma_start(out=out[c * P : (c + 1) * P, :], in_=result[c][:])
+        def store(c, source, lo=0, hi=V):
+            nc.sync.dma_start(out=out[c * P : (c + 1) * P, lo:hi], in_=source[:, lo:hi])
 
-        first = keep.tile([P, 2, V], F32, name="first", tag="w_raw1", align_bytes=64)
-        for d in (1, 2):
-            fetched[0, d] = first[:, d - 1]
-
-        fetch_plain(0, 0, fresh(0, 0))
-        plain0 = [turn_sum(0, (0,), 0)]
-        activate(1, 0, S, acc1)
-        fetch_plain(0, 3, fresh(0, 3))
-        plain0.append(turn_sum(0, (3,), 1))
-        extra = keep.tile([P, P], F32, name="extra")
-        nc.scalar.activation(extra[:], y[1][:].indirect(pos_t[0][:, 0:8]), COPY)
-        activate(2, 0, S, acc2)
-        for d in (1, 2):
-            fetch_gated(0, d, fetched[0, d])
-        turned0 = turn_sum(0, (1, 2), 2)
-        w_grp3 = keep.tile([P, P, PACK], BF16, name="w_grp3", tag="x_grp1", align_bytes=64)
-        interleave_w(3, nc.vector.tensor_copy, w_grp3[:])
-        rest = keep.tile([P, P], F32, name="rest")
-        nc.vector.tensor_tensor(rest[:], y[1][:].indirect(pos_t[0][:, 8:16]), gates[0][:, 0, P:V], MULT)
-        quantize_w(3)
+        for c in range(2):
+            w_grp[c] = sbuf("w_grp%d" % c, [P, P, PACK], BF16)
+        interleave_w(0, 0, P, nc.vector.tensor_copy)
+        interleave_w(1, 0, P, nc.scalar.copy)
+        x_scales = sbuf("x_scales", [P, S], U8, "w_raw0")
+        quantize_w(0, 0, P)
+        pieces = (HALF, HALF + P, 0, P)
+        for lo in pieces:
+            quantize_x(lo, lo + P)
+        for i, lo in enumerate(pieces):
+            activate(0, lo, lo + P, product(0, lo, lo + P, i))
+        quantize_w(1, 0, P)
+        acc1 = [product(1, h * HALF, (h + 1) * HALF, 4 + h) for h in range(2)]
+        pair_w = sbuf("pair_w", [P, 2, P, PACK], BF16, "w_raw1")
+        for c in (2, 3):
+            w_grp[c] = pair_w[:, c - 2]
+            interleave_w(c, 0, P, nc.vector.tensor_copy)
+        for c in (2, 3):
+            quantize_w(c, 0, P)
+        acc2 = product(2, 0, S, 6)
         acc3 = product(3, 0, S, 7)
-        late = keep.tile([P, 9, V], F32, name="late", tag="x_codes", align_bytes=64)
-        fetch_plain(2, 0, fresh(2, 0))
-        activate(3, 0, S, acc3)
-        extra_turned = bank(7, [P, P])
-        nc.tensor.transpose(extra_turned[:], extra[:], ident[:])
-        plain2 = [turn_sum(2, (0,), 4)]
-        for d in (1, 2):
-            fetch_gated(1, d, fresh(1, d))
-        turned1 = bank(5, [P, V])
-        nc.tensor.matmul(turned1[:, P:V], rest[:], ident[:], start=True, stop=False, is_transpose=True)
-        for d in (1, 2):
-            turn(turned1, fetched[1, d], False, d == 2)
-        fetch_gated(1, 3, fresh(1, 3))
-        sum1 = keep.tile([P, V], F32, name="sum1")
-        extra_scaled = keep.tile([P, P], F32, name="extra_scaled", tag="w_scales3", align_bytes=64)
-        nc.scalar.activation(extra_scaled[:], extra_turned[:], COPY, scale=consts[:, 0, 0:1])
-        empty_sum(sum1[:], turned1)
-        back1 = bank(5, [P, V])
-        nc.tensor.matmul(back1[:, 0:P], extra_scaled[:], ident[:], start=True, stop=False, is_transpose=True)
-        turn(back1, sum1[:], False, True)
+        for h in range(2):
+            activate(1, h * HALF, (h + 1) * HALF, acc1[h])
+        g00 = fetch_gated(0, 0, row("g00", "w_raw2"))
+
+        plain0 = sbuf("plain0", [P, 3, V], F32, "w_codes1")
+        mid = sbuf("mid", [P, 2, V], F32, "w_codes2")
+        late = sbuf("late", [P, 3, V], F32, "x_codes")
+        sum1 = bank(5, [P, V])
+        t01 = turned(fetch_plain(0, 1, plain0[:, 0]), 0)
+        turn(sum1, fetch_gated(1, 0, row("g10")), True, False)
+        t02 = turned(fetch_plain(0, 2, plain0[:, 1]), 1)
+        turn(sum1, fetch_gated(1, 1, row("g11")), False, False)
+        g03 = fetch_plain(0, 3, plain0[:, 2])
+        t03 = [bank(number, [P, P]) for number in (2, 4)]
+        for h in range(2):
+            turn_half(t03[h][:], g03, h, True, True)
+        activate(2, 0, S, acc2)
+        gated = sbuf("gated", [P, 2, V], F32, "w_raw3")
+        early2 = sbuf("early2", [P, 2, V], F32, "w_raw1")
+        turn(sum1, fetch_gated(1, 2, gated[:, 0]), False, False)
         back0 = bank(3, [P, V])
-        for i, d in enumerate((0, 3)):
-            turn(back0, empty_scaled(late[:, i], d, plain0[i]), i == 0, False)
-        turn(back0, empty_sum(late[:, 2], turned0), False, True)
-        fetch_plain(2, 1, late[:, 3])
-        plain2.append(turn_sum(2, (1,), 0))
-        fetch_plain(2, 2, late[:, 5])
-        plain2.append(turn_sum(2, (2,), 1))
-        back2 = bank(6, [P, V])
-        nc.scalar.copy(result[0][:], back0[:])
-        store(0)
+        turn(back0, scaled(1, t01, mid[:, 0]), True, False)
+        turn(sum1, fetch_gated(1, 3, gated[:, 1]), False, True)
+        turn(back0, scaled(2, t02, mid[:, 1]), False, False)
+        activate(3, 0, S, acc3)
+        g20 = fetch_gated(2, 0, early2[:, 0])
+        scaled03 = row("scaled03", "w_scales3")
+        nc.scalar.activation(scaled03[:, 0:P], t03[0][:], COPY, scale=consts[:, 0, 3:4])
+        nc.vector.tensor_scalar(scaled03[:, P:V], t03[1][:], consts[:, 1, 3:4], None, MULT)
+        turn(back0, scaled03, False, True)
+        g21 = fetch_gated(2, 1, early2[:, 1])
+        nc.scalar.copy(late[:, 0], sum1[:])
+        late2 = sbuf("late2", [P, 3, V], F32, "w_codes1")
+        t30 = turned(fetch_plain(3, 0, late[:, 1]), 0)
+        g22 = fetch_gated(2, 2, late2[:, 0])
+        pair2 = add(late2[:, 1], g20, g21)
+        t31 = turned(fetch_plain(3, 1, late[:, 2]), 1)
+        g23 = fetch_gated(2, 3, late2[:, 2])
+        three2 = add(row("three2"), pair2, g22)
+        result0 = add(row("result0"), g00, back0[:])
+        store(0, result0)
+        closing = sbuf("closing", [P, 2, V], F32, "w_scales3")
+        result2 = add(closing[:, 0], three2, g23)
+        store(2, result2)
+        g32 = fetch_plain(3, 2, row("g32", "w_codes3"))
+        t32 = [bank(number, [P, P]) for number in (2, 6)]
+        for h in range(2):
+            turn_half(t32[h][:], g32, h, True, True)
+        g33 = closing[:, 1]
+        fetch_gated(3, 3, g33, 0, P)
+        fetch_gated(3, 3, g33, P, V)
+        back3 = [bank(number, [P, P]) for number in (4, 7)]
+        halves = [[t30[:, 0:P], t30[:, P:V]], [t31[:, 0:P], t31[:, P:V]], [t32[0][:], t32[1][:]]]
         for d in range(3):
-            turn(back2, empty_scaled(late[:, 6 + d], d, plain2[d]), d == 0, d == 2)
-        for d in range(3):
-            fetch_gated(3, d, fresh(3, d))
-        partial = [keep.tile([P, V], F32, name="partial%d" % i) for i in range(2)]
-        nc.vector.tensor_tensor(partial[0][:], fetched[3, 0], fetched[3, 1], ADD)
-        fetch_gated(3, 3, fresh(3, 3))
-        nc.vector.tensor_tensor(partial[1][:], partial[0][:], fetched[3, 2], ADD)
-        nc.vector.tensor_tensor(result[1][:], fetched[1, 3], back1[:], ADD)
-        store(1)
-        closing = keep.tile([P, V], F32, name="closing", tag="sum1")
-        fetch_gated(2, 3, closing[:])
-        result.append(keep.tile([P, V], F32, name="result3", tag="fetched1_3"))
-        nc.vector.tensor_tensor(result[3][:], partial[1][:], fetched[3, 3], ADD)
-        store(3)
+            for h in range(2):
+                part = sbuf("scaled3%d_%d" % (d, h), [P, P])
+                nc.scalar.activation(part[:], halves[d][h], COPY, scale=consts[:, h, d : d + 1])
+                if (d, h) == (0, 1):
+                    back1 = turned(late[:, 0], 0)
+                turn_half(back3[h][:], part, 0, d == 0, d == 2)
+        result1 = row("result1", "scaled31_0")
+        nc.scalar.copy(result1, back1[:])
+        store(1, result1)
+        result3 = row("result3")
         for h in range(2):
             cut = slice(h * P, (h + 1) * P)
-            nc.vector.tensor_tensor(result[2][:, cut], closing[:, cut], back2[:, cut], ADD)
-            nc.sync.dma_start(out=out[2 * P : 3 * P, cut], in_=result[2][:, cut])
+            add(result3[:, cut], g33[:, cut], back3[h][:])
+            store(3, result3, h * P, (h + 1) * P)

from contextlib import ExitStack

import concourse.mybir as mybir
from concourse.masks import make_identity

K, T, D, S, V, N = 512, 2048, 4, 512, 256, 512
FLOPS = 2 * K * N * S

F32 = mybir.dt.float32
BF16 = mybir.dt.bfloat16
U32 = mybir.dt.uint32
U16 = mybir.dt.uint16
U8 = mybir.dt.uint8
FP8X4 = mybir.dt.float8_e4m3fn_x4
GELU = mybir.ActivationFunctionType.Gelu_apprx_tanh
COPY = mybir.ActivationFunctionType.Copy
MULT = mybir.AluOpType.mult
ADD = mybir.AluOpType.add

P = 128
PACK = 4
BLOCKS = N // P
HALF = S // 2
PER_COLUMN = 16
FIRST_SPLIT = 1408


def tile_picked_sub_lin_gelu_sub_e_kernel(tc, xT, w, b, gate, offs, pos1, pos2, pos3, pos4, out):
    nc = tc.nc
    with ExitStack() as ctx:
        lists = ctx.enter_context(tc.tile_pool(name="lists", bufs=1))
        keep = ctx.enter_context(tc.tile_pool(name="keep", bufs=1))
        psum = ctx.enter_context(tc.psum_pool(name="psum", bufs=1))

        def bank(number, shape):
            return psum.tile(shape, F32, name="bank", tag="bank%d" % number)

        def sbuf(name, shape, dtype=F32, tag=None):
            return keep.tile(shape, dtype, name=name, tag=tag or name, align_bytes=64)

        offs_t = lists.tile([P, S // PER_COLUMN], U16, name="offs_t")
        pos_t = [lists.tile([P, V // PER_COLUMN], U16, name="pos_t%d" % d) for d in range(D)]
        pos_in = [pos1, pos2, pos3, pos4]

        x_raw = [sbuf("x_raw%d" % t, [P, T]) for t in range(PACK)]
        w_raw = [sbuf("w_raw%d" % c, [P, PACK, P]) for c in range(BLOCKS)]
        x_rows = xT.rearrange("(p j) c -> p j c", j=PACK)
        w_rows = w.rearrange("(p j) m -> p j m", j=PACK)

        def load_w(c):
            nc.sync.dma_start(out=w_raw[c][:], in_=w_rows[:, :, c * P : (c + 1) * P])

        def load_pos(d):
            nc.sync.dma_start(pos_t[d][:], pos_in[d])

        rows = sbuf("rows", [P, V])
        nc.gpsimd.memset(rows[:], 0.0)

        nc.scalar.dma_start(out=x_raw[0][:, 0:FIRST_SPLIT], in_=x_rows[:, 0, 0:FIRST_SPLIT])
        nc.sync.dma_start(out=x_raw[0][:, FIRST_SPLIT:T], in_=x_rows[:, 0, FIRST_SPLIT:T])
        nc.sync.dma_start(offs_t[:], offs)
        nc.sync.dma_start(out=x_raw[1][:], in_=x_rows[:, 1, :])
        nc.sync.dma_start(out=rows[0:D, :], in_=gate[:, 0, :])
        nc.sync.dma_start(out=rows[D : D + BLOCKS, 0:P], in_=b.rearrange("(c m) o -> c (m o)", c=BLOCKS))
        nc.sync.dma_start(out=x_raw[2][:], in_=x_rows[:, 2, :])
        nc.sync.dma_start(out=x_raw[3][:], in_=x_rows[:, 3, :])
        load_pos(0)
        load_w(0)
        load_w(1)
        load_w(2)
        load_w(3)
        load_pos(1)
        load_pos(2)
        load_pos(3)

        warm_out = sbuf("warm_out", [P, 8])
        nc.scalar.activation(warm_out[32:64, :], rows[32:64, 0:8], GELU)

        ident = sbuf("ident", [P, P])
        make_identity(nc, ident[:])
        rows_turned = bank(7, [P, 2, P])
        for h in range(2):
            nc.tensor.transpose(rows_turned[:, h, :], rows[:, h * P : (h + 1) * P], ident[:])
        consts = sbuf("consts", [P, 2, D + BLOCKS])
        nc.scalar.copy(consts[:], rows_turned[:, :, 0 : D + BLOCKS])
        gates = [sbuf("gates%d" % i, [P, 2, V]) for i in range(2)]
        for i in range(2):
            spread = bank(5 + i, [P, 2, V])
            for j in range(2):
                for h in range(2):
                    column = consts[:, h, 2 * i + j : 2 * i + j + 1].to_broadcast([P, P])
                    nc.tensor.transpose(spread[:, j, h * P : (h + 1) * P], column, ident[:])
            nc.scalar.copy(gates[i][:], spread[:])

        x_grp = [sbuf("x_grp%d" % h, [P, HALF, PACK], BF16) for h in range(2)]
        cols = HALF // PER_COLUMN
        for t in range(PACK):
            nc.vector.tensor_copy(x_grp[0][:, :, t], x_raw[t][:].indirect(offs_t[:, 0:cols]))
            nc.scalar.activation(x_grp[1][:, :, t], x_raw[t][:].indirect(offs_t[:, cols : 2 * cols]), COPY)

        x_codes = sbuf("x_codes", [P, S], U32)
        w_codes = [sbuf("w_codes%d" % c, [P, P], U32) for c in range(BLOCKS)]
        w_scales = [sbuf("w_scales%d" % c, [P, P], U8) for c in range(BLOCKS)]
        w_grp = {}
        y = [sbuf("y%d" % c, [P, S]) for c in range(BLOCKS)]

        def quantize_x(lo, hi):
            nc.vector.quantize_mx(
                out=x_codes[:, lo:hi].bitcast(FP8X4),
                scales=x_scales[:, lo:hi],
                in_=x_grp[lo // HALF][:, lo % HALF : lo % HALF + hi - lo, :].rearrange("p s j -> p (s j)"),
            )

        def interleave_w(c, lo, hi, copy):
            copy(
                w_grp[c][:, lo:hi, :].rearrange("p (m i) j -> p m j i", i=4),
                w_raw[c][:, :, lo:hi].rearrange("p j (m i) -> p m j i", i=4),
            )

        def quantize_w(c, lo, hi):
            nc.vector.quantize_mx(
                out=w_codes[c][:, lo:hi].bitcast(FP8X4),
                scales=w_scales[c][:, lo:hi],
                in_=w_grp[c][:, lo:hi, :].rearrange("p m j -> p (m j)"),
            )

        def product(c, lo, hi, number):
            acc = bank(number, [P, hi - lo])
            nc.tensor.matmul_mx(
                out=acc[:],
                lhsT=w_codes[c][:].bitcast(FP8X4),
                lhsT_scale=w_scales[c][:],
                rhs=x_codes[:, lo:hi].bitcast(FP8X4),
                rhs_scale=x_scales[:, lo:hi],
                start=True,
                stop=True,
            )
            return acc

        def activate(c, lo, hi, acc):
            nc.scalar.activation(y[c][:, lo:hi], acc[:], GELU, bias=consts[:, 0, D + c : D + c + 1])

        def fetch_gated(c, d, into, lo=0, hi=V):
            offsets = pos_t[d][:, lo // PER_COLUMN : hi // PER_COLUMN]
            nc.vector.tensor_tensor(into[:, lo:hi], y[c][:].indirect(offsets), gates[d // 2][:, d % 2, lo:hi], MULT)
            return into

        def fetch_plain(c, d, into):
            nc.scalar.activation(into, y[c][:].indirect(pos_t[d][:]), COPY)
            return into

        def turn_half(target, source, h, start, stop):
            nc.tensor.matmul(target, source[:, h * P : (h + 1) * P], ident[:], start=start, stop=stop, is_transpose=True)

        def turn(target, source, first_pass, last_pass):
            for h in range(2):
                turn_half(target[:, h * P : (h + 1) * P], source, h, first_pass and h == 0, last_pass and h == 1)

        def turned(source, number):
            target = bank(number, [P, V])
            turn(target, source, True, True)
            return target

        def scaled(d, source, into):
            for h in range(2):
                cut = slice(h * P, (h + 1) * P)
                nc.scalar.activation(into[:, cut], source[:, cut], COPY, scale=consts[:, h, d : d + 1])
            return into

        def row(name, tag=None):
            return sbuf(name, [P, V], F32, tag)[:]

        def add(into, first, second):
            nc.vector.tensor_tensor(into, first, second, ADD)
            return into

        def store(c, source, lo=0, hi=V):
            nc.sync.dma_start(out=out[c * P : (c + 1) * P, lo:hi], in_=source[:, lo:hi])

        for c in range(2):
            w_grp[c] = sbuf("w_grp%d" % c, [P, P, PACK], BF16)
        interleave_w(0, 0, P, nc.vector.tensor_copy)
        interleave_w(1, 0, P, nc.scalar.copy)
        x_scales = sbuf("x_scales", [P, S], U8, "w_raw0")
        quantize_w(0, 0, P)
        pieces = (HALF, HALF + P, 0, P)
        for lo in pieces:
            quantize_x(lo, lo + P)
        for i, lo in enumerate(pieces):
            activate(0, lo, lo + P, product(0, lo, lo + P, i))
        quantize_w(1, 0, P)
        acc1 = [product(1, h * HALF, (h + 1) * HALF, 4 + h) for h in range(2)]
        pair_w = sbuf("pair_w", [P, 2, P, PACK], BF16, "w_raw1")
        for c in (2, 3):
            w_grp[c] = pair_w[:, c - 2]
            interleave_w(c, 0, P, nc.vector.tensor_copy)
        for c in (2, 3):
            quantize_w(c, 0, P)
        acc2 = product(2, 0, S, 6)
        acc3 = product(3, 0, S, 7)
        for h in range(2):
            activate(1, h * HALF, (h + 1) * HALF, acc1[h])
        g00 = fetch_gated(0, 0, row("g00", "w_raw2"))

        plain0 = sbuf("plain0", [P, 3, V], F32, "w_codes1")
        mid = sbuf("mid", [P, 2, V], F32, "w_codes2")
        late = sbuf("late", [P, 3, V], F32, "x_codes")
        sum1 = bank(5, [P, V])
        t01 = turned(fetch_plain(0, 1, plain0[:, 0]), 0)
        turn(sum1, fetch_gated(1, 0, row("g10")), True, False)
        t02 = turned(fetch_plain(0, 2, plain0[:, 1]), 1)
        turn(sum1, fetch_gated(1, 1, row("g11")), False, False)
        g03 = fetch_plain(0, 3, plain0[:, 2])
        t03 = [bank(number, [P, P]) for number in (2, 4)]
        for h in range(2):
            turn_half(t03[h][:], g03, h, True, True)
        activate(2, 0, S, acc2)
        gated = sbuf("gated", [P, 2, V], F32, "w_raw3")
        early2 = sbuf("early2", [P, 2, V], F32, "w_raw1")
        turn(sum1, fetch_gated(1, 2, gated[:, 0]), False, False)
        back0 = bank(3, [P, V])
        turn(back0, scaled(1, t01, mid[:, 0]), True, False)
        turn(sum1, fetch_gated(1, 3, gated[:, 1]), False, True)
        turn(back0, scaled(2, t02, mid[:, 1]), False, False)
        activate(3, 0, S, acc3)
        g20 = fetch_gated(2, 0, early2[:, 0])
        scaled03 = row("scaled03", "w_scales3")
        nc.scalar.activation(scaled03[:, 0:P], t03[0][:], COPY, scale=consts[:, 0, 3:4])
        nc.vector.tensor_scalar(scaled03[:, P:V], t03[1][:], consts[:, 1, 3:4], None, MULT)
        turn(back0, scaled03, False, True)
        g21 = fetch_gated(2, 1, early2[:, 1])
        nc.scalar.copy(late[:, 0], sum1[:])
        late2 = sbuf("late2", [P, 3, V], F32, "w_codes1")
        t30 = turned(fetch_plain(3, 0, late[:, 1]), 0)
        g22 = fetch_gated(2, 2, late2[:, 0])
        pair2 = add(late2[:, 1], g20, g21)
        t31 = turned(fetch_plain(3, 1, late[:, 2]), 1)
        g23 = fetch_gated(2, 3, late2[:, 2])
        three2 = add(row("three2"), pair2, g22)
        result0 = add(row("result0"), g00, back0[:])
        store(0, result0)
        closing = sbuf("closing", [P, 2, V], F32, "w_scales3")
        result2 = add(closing[:, 0], three2, g23)
        store(2, result2)
        g32 = fetch_plain(3, 2, row("g32", "w_codes3"))
        t32 = [bank(number, [P, P]) for number in (2, 6)]
        for h in range(2):
            turn_half(t32[h][:], g32, h, True, True)
        g33 = closing[:, 1]
        fetch_gated(3, 3, g33, 0, P)
        fetch_gated(3, 3, g33, P, V)
        back3 = [bank(number, [P, P]) for number in (4, 7)]
        halves = [[t30[:, 0:P], t30[:, P:V]], [t31[:, 0:P], t31[:, P:V]], [t32[0][:], t32[1][:]]]
        for d in range(3):
            for h in range(2):
                part = sbuf("scaled3%d_%d" % (d, h), [P, P])
                nc.scalar.activation(part[:], halves[d][h], COPY, scale=consts[:, h, d : d + 1])
                if (d, h) == (0, 1):
                    back1 = turned(late[:, 0], 0)
                turn_half(back3[h][:], part, 0, d == 0, d == 2)
        result1 = row("result1", "scaled31_0")
        nc.scalar.copy(result1, back1[:])
        store(1, result1)
        result3 = row("result3")
        for h in range(2):
            cut = slice(h * P, (h + 1) * P)
            add(result3[:, cut], g33[:, cut], back3[h][:])
            store(3, result3, h * P, (h + 1) * P)
